import numpy as np
import ml_dtypes


def mxq(x, axis, fmt="e4m3"):
    dtype, down = {"e4m3": (ml_dtypes.float8_e4m3fn, 7), "e5m2": (ml_dtypes.float8_e5m2, 14)}[fmt]
    v = np.moveaxis(np.asarray(x, np.float32).astype(ml_dtypes.bfloat16).astype(np.float64), axis, -1)
    blocks = v.reshape(v.shape[:-1] + (-1, 32))
    amax = np.abs(blocks).max(-1, keepdims=True)
    byte = np.maximum(np.where(amax > 0, np.frexp(amax)[1] - 1 + 127, 0) - down, 1)
    scale = np.exp2(byte - 127.0)
    codes = (blocks / scale).astype(np.float32).astype(dtype).astype(np.float64)
    return np.moveaxis((codes * scale).reshape(v.shape), -1, axis)


WIDE = False


def mx_kscale(k):
    if not WIDE:
        return np.ones(k)
    levels = np.array([30, -30])
    if k % 512:
        return np.exp2(np.random.permutation(np.resize(levels, k // 32))).repeat(32)
    a = np.empty((k // 512, 16))
    for p in range(k // 512):
        a[p, :8] = np.random.permutation(np.resize(levels, 8))
        for g in range(8):
            far = levels[np.abs(levels - a[p, g]) >= 10]
            a[p, g + 8] = far[np.random.randint(len(far))]
    return np.exp2(a.ravel()).repeat(32)


def f64(x):
    return np.asarray(x).astype(np.float64)


def striped(idx):
    return np.tile(idx.reshape(-1, 16).T, (8, 1)).astype(np.uint16)


def unstriped(offs):
    return offs[:16].T.reshape(-1).astype(np.int64)


def bf(x):
    return np.asarray(x, np.float32).astype(ml_dtypes.bfloat16)


E2M1 = np.array([0.0, 0.5, 1.0, 1.5, 2.0, 3.0, 4.0, 6.0, -0.0, -0.5, -1.0, -1.5, -2.0, -3.0, -4.0, -6.0])


def pack_weight(w, fmt):
    k, n = w.shape
    w = f64(bf(w)).reshape(k // 32, 32, n)
    amax = np.abs(w).max(1)
    if fmt in ("e4m3", "e5m2"):
        byte = np.frexp(amax)[1] - 1 + 127 - (7 if fmt == "e4m3" else 14)
    else:
        mant, ex = np.frexp(amax / 6.0)
        byte = np.where(mant > 0.5, ex, ex - 1) + 127
    byte = np.clip(np.where(amax > 0, byte, 1), 1, 254)
    scaled = (w * np.exp2(127.0 - byte)[:, None, :]).reshape(k, n).astype(np.float32)
    by_word = np.ascontiguousarray(scaled.reshape(k // 512, 128, 4, n).transpose(0, 1, 3, 2))
    if fmt in ("e4m3", "e5m2"):
        words = by_word.astype(ml_dtypes.float8_e4m3fn if fmt == "e4m3" else ml_dtypes.float8_e5m2).view(np.uint8)
    else:
        c = by_word.astype(ml_dtypes.float4_e2m1fn).view(np.uint8) & 0xF
        words = c[..., 0::2] | (c[..., 1::2] << 4)
    return np.ascontiguousarray(words), np.ascontiguousarray(byte.astype(np.uint8).reshape(k // 512, 16, n))


def unpack_weight(words, scales, fmt):
    g, p, n, _ = words.shape
    if fmt in ("e4m3", "e5m2"):
        vals = np.ascontiguousarray(words).view(ml_dtypes.float8_e4m3fn if fmt == "e4m3" else ml_dtypes.float8_e5m2).astype(np.float64)
    else:
        nib = np.empty((g, p, n, 4), np.uint8)
        nib[..., 0::2] = words & 0xF
        nib[..., 1::2] = words >> 4
        vals = E2M1[nib]
    vals = vals * np.repeat(np.exp2(scales.astype(np.float64) - 127.0), 8, axis=1)[..., None]
    return vals.transpose(0, 1, 3, 2).reshape(g * 512, n)


K, T, S, H, N = 1536, 2048, 1024, 512, 1536

def setup_inputs():
    n = np.random.standard_normal
    s = mx_kscale(K)[:, None]
    u = mx_kscale(H)[:, None]
    shocks = n((K, T)) * np.exp(0.6 * n((1, T))) * s
    tab_words, tab_scales = pack_weight(shocks, "e5m2")
    w4_words, w4_scales = pack_weight(n((H, N)) / np.sqrt(H) / u, "e4m3")
    return {
        "tab_words": tab_words,
        "tab_scales": tab_scales,
        "offs": striped(np.random.permutation(T)[:S]),
        "w1": (n((K, H)) / np.sqrt(K) / s).astype(np.float32),
        "gain": (np.exp(0.3 * n(H)) * u[:, 0]).astype(np.float32),
        "w4_words": w4_words,
        "w4_scales": w4_scales,
        "spec": (0.5 * np.exp(0.3 * n(N))).astype(np.float32),
    }

def reference(tab_words, tab_scales, offs, w1, gain, w4_words, w4_scales, spec):
    v = unpack_weight(tab_words, tab_scales, "e5m2")[:, unstriped(offs)]
    w1q = mxq(f64(w1), 0, "e4m3")
    f = w1q.T @ v
    h = f64(gain)[:, None] * np.square(f)
    hq = mxq(h, 0, "e4m3")
    w4 = unpack_weight(w4_words, w4_scales, "e4m3")
    y = w4.T @ hq
    return np.sqrt(np.abs(y) + f64(spec)[:, None])

@@ -1,0 +1,193 @@
+from contextlib import ExitStack
+
+import concourse.mybir as mybir
+
+K, T, S, H, N = 1536, 2048, 1024, 512, 1536
+FLOPS = 2 * K * H * S + 2 * H * N * S
+
+F32 = mybir.dt.float32
+BF16 = mybir.dt.bfloat16
+I32 = mybir.dt.int32
+U32 = mybir.dt.uint32
+U16 = mybir.dt.uint16
+U8 = mybir.dt.uint8
+E4M3 = mybir.dt.float8_e4m3fn_x4
+E5M2 = mybir.dt.float8_e5m2_x4
+ACT = mybir.ActivationFunctionType
+ALU = mybir.AluOpType
+
+P = 128
+PACK = 4
+PASSES = K // (P * PACK)
+COLS = 512
+HALVES = S // COLS
+N_TILES = N // P
+CHUNK = 256
+MOVED_ROWS = 100
+FIRST_ROW = 32 - 4 * PASSES
+
+
+def tile_list_shock_factor_vols_kernel(tc, tab_words, tab_scales, offs, w1, gain, w4_words, w4_scales, spec, out):
+    nc = tc.nc
+    with ExitStack() as ctx:
+        keep = ctx.enter_context(tc.tile_pool(name="keep", bufs=1))
+        ring = ctx.enter_context(tc.tile_pool(name="ring", bufs=4))
+        psum = ctx.enter_context(tc.psum_pool(name="psum", bufs=1))
+
+        offsets = keep.tile([P, S // 16], U16, name="offsets")
+        nc.sync.dma_start(offsets[:], offs)
+
+        tab_plane = keep.tile([P, T], U8, name="tab_plane", align_bytes=64)
+        for q in range(4):
+            nc.vector.memset(tab_plane[32 * q : 32 * q + FIRST_ROW, :].bitcast(I32), 0)
+        picked = keep.tile([P, S], U8, name="picked", align_bytes=64)
+        v_planes = [keep.tile([P, S], U8, name=f"v_plane{a}", align_bytes=64) for a in range(PASSES)]
+        for a in range(PASSES):
+            nc.vector.memset(v_planes[a][:].bitcast(I32), 0)
+        w4_plane = keep.tile([P, N], U8, name="w4_plane", align_bytes=64)
+        nc.vector.memset(w4_plane[:].bitcast(I32), 0)
+
+        tabs = [keep.tile([P, T], I32, name=f"tab{a}", align_bytes=64) for a in range(PASSES)]
+        raws = [keep.tile([P, PACK, H], F32, name=f"w1_raw{a}", align_bytes=64) for a in range(PASSES)]
+
+        def load_tab(a, queue):
+            queue.dma_start(out=tabs[a][:], in_=tab_words[a].rearrange("p t i -> p (t i)").bitcast(I32))
+
+        def load_w1(a):
+            rows = w1[a * P * PACK : (a + 1) * P * PACK, :]
+            nc.sync.dma_start(out=raws[a][:], in_=rows.rearrange("(p j) c -> p j c", j=PACK))
+
+        load_tab(0, nc.scalar)
+        load_tab(1, nc.scalar)
+        for q in range(4):
+            nc.sync.dma_start(
+                out=tab_plane[32 * q + FIRST_ROW : 32 * q + 32, :].bitcast(I32),
+                in_=tab_scales[:, 4 * q : 4 * q + 4, :].bitcast(I32),
+            )
+        load_w1(0)
+        load_w1(1)
+        load_w1(2)
+        load_tab(2, nc.sync)
+        warm = keep.tile([P, 1], F32, name="warm")
+        warm_out = keep.tile([P, 1], F32, name="warm_out")
+        nc.vector.memset(warm[:], 1.0)
+        nc.scalar.activation(out=warm_out[:], in_=warm[:], func=ACT.Sqrt)
+
+        gain_sb = keep.tile([P, PACK], F32, name="gain_sb")
+        nc.sync.dma_start(out=gain_sb[:], in_=gain.rearrange("(p t) -> p t", t=PACK))
+        w4_codes = keep.tile([P, N], I32, name="w4_codes", align_bytes=64)
+        nc.sync.dma_start(out=w4_codes[:], in_=w4_words[0].rearrange("p c i -> p (c i)").bitcast(I32))
+        spec_sb = keep.tile([P, N_TILES], F32, name="spec_sb")
+        with nc.allow_non_contiguous_dma(reason="one value of spec for each partition and tile of rows"):
+            nc.sync.dma_start(out=spec_sb[:], in_=spec.rearrange("(c p) -> p c", p=P))
+        for q in range(4):
+            nc.sync.dma_start(
+                out=w4_plane[32 * q : 32 * q + 4, :].bitcast(I32),
+                in_=w4_scales[0, 4 * q : 4 * q + 4, :].bitcast(I32),
+            )
+
+        v_codes = [[keep.tile([P, COLS], U32, name=f"v_codes{a}_{h}", align_bytes=64) for h in range(HALVES)] for a in range(PASSES)]
+        grouped = [keep.tile([P, H * PACK], BF16, name=f"w1_grouped{a}", align_bytes=64) for a in range(PASSES)]
+        w1_codes = [keep.tile([P, H], U32, name=f"w1_codes{a}", align_bytes=64) for a in range(PASSES)]
+        w1_planes = [keep.tile([P, H], U8, name=f"w1_plane{a}", align_bytes=64) for a in range(PASSES)]
+        f_banks = [[psum.tile([P, COLS], F32, name=f"f{h}_{t}", tag=f"bank{PACK * h + t}") for t in range(PACK)] for h in range(HALVES)]
+
+        def gather_words(a, h):
+            cols = COLS // 16
+            nc.vector.tensor_copy(out=v_codes[a][h][:], in_=tabs[a][:].bitcast(U32).indirect(offsets[:, h * cols : (h + 1) * cols]))
+
+        def gather_scales():
+            nc.vector.tensor_copy(out=picked[:], in_=tab_plane[:].indirect(offsets[:]))
+            for a in range(PASSES):
+                nc.gpsimd.dma_start(
+                    out=v_planes[a][0:MOVED_ROWS, :].bitcast(I32),
+                    in_=picked[FIRST_ROW + 4 * a : FIRST_ROW + 4 * a + MOVED_ROWS, :].bitcast(I32),
+                )
+
+        def cast_w1(a, copy):
+            copy(
+                out=grouped[a][:].rearrange("p (t m j) -> p m j t", t=PACK, j=PACK),
+                in_=raws[a][:].rearrange("p j (m t) -> p m j t", t=PACK),
+            )
+
+        def quantize_w1(a):
+            nc.vector.quantize_mx(out=w1_codes[a][:].bitcast(E4M3), scales=w1_planes[a][:], in_=grouped[a][:])
+
+        def first_product(a, h):
+            for t in range(PACK):
+                nc.tensor.matmul_mx(
+                    out=f_banks[h][t][:],
+                    lhsT=w1_codes[a][:, t * P : (t + 1) * P].bitcast(E4M3),
+                    lhsT_scale=w1_planes[a][:, t * P : (t + 1) * P],
+                    rhs=v_codes[a][h][:].bitcast(E5M2),
+                    rhs_scale=v_planes[a][:, h * COLS : (h + 1) * COLS],
+                    start=(a == 0),
+                    stop=(a == PASSES - 1),
+                )
+
+        gather_words(0, 0)
+        gather_words(0, 1)
+        gather_scales()
+        gather_words(1, 0)
+        gather_words(1, 1)
+        cast_w1(0, nc.scalar.copy)
+        quantize_w1(0)
+        first_product(0, 0)
+        first_product(0, 1)
+        cast_w1(1, nc.scalar.copy)
+        cast_w1(2, nc.vector.tensor_copy)
+        quantize_w1(1)
+        first_product(1, 0)
+        first_product(1, 1)
+        quantize_w1(2)
+        for h in range(HALVES):
+            gather_words(2, h)
+            first_product(2, h)
+
+        squares = [keep.tile([P, PACK, COLS], F32, name=f"squares{h}", align_bytes=64) for h in range(HALVES)]
+        h_grouped = [keep.tile([P, COLS * PACK], BF16, name=f"h_grouped{h}", align_bytes=64) for h in range(HALVES)]
+        h_codes = [keep.tile([P, COLS], U32, name=f"h_codes{h}", align_bytes=64) for h in range(HALVES)]
+        h_planes = [keep.tile([P, COLS], U8, name=f"h_plane{h}", align_bytes=64) for h in range(HALVES)]
+        gain_rows = gain_sb[:].unsqueeze(1).unsqueeze(3).to_broadcast([P, CHUNK // 4, PACK, 4])
+
+        for h, width in enumerate((CHUNK, COLS)):
+            for c0 in range(0, COLS, width):
+                for t in range(PACK):
+                    nc.scalar.activation(out=squares[h][:, t, c0 : c0 + width], in_=f_banks[h][t][:, c0 : c0 + width], func=ACT.Square)
+        for h in range(HALVES):
+            for c0 in range(0, COLS, CHUNK):
+                nc.vector.tensor_tensor(
+                    out=h_grouped[h][:, c0 * PACK : (c0 + CHUNK) * PACK].rearrange("p (c i t) -> p c t i", i=4, t=PACK),
+                    in0=squares[h][:, :, c0 : c0 + CHUNK].rearrange("p t (c i) -> p c t i", i=4),
+                    in1=gain_rows,
+                    op=ALU.mult,
+                )
+            for c0 in range(0, COLS, CHUNK):
+                nc.vector.quantize_mx(
+                    out=h_codes[h][:, c0 : c0 + CHUNK].bitcast(E4M3),
+                    scales=h_planes[h][:, c0 : c0 + CHUNK],
+                    in_=h_grouped[h][:, c0 * PACK : (c0 + CHUNK) * PACK],
+                )
+
+        for i in range(HALVES * N_TILES):
+            h, c = divmod(i, N_TILES)
+            y = psum.tile([P, COLS], F32, name=f"y{i}", tag=f"bank{i % 8}")
+            nc.tensor.matmul_mx(
+                out=y[:],
+                lhsT=w4_codes[:, c * P : (c + 1) * P].bitcast(E4M3),
+                lhsT_scale=w4_plane[:, c * P : (c + 1) * P],
+                rhs=h_codes[h][:].bitcast(E4M3),
+                rhs_scale=h_planes[h][:],
+                start=True,
+                stop=True,
+            )
+            size = ring.tile([P, COLS], F32, name="size")
+            if i < 3 or i % 3 == 2:
+                nc.scalar.activation(out=size[:], in_=y[:], func=ACT.Abs)
+            else:
+                y_sb = ring.tile([P, COLS], F32, name="y_sb")
+                nc.vector.tensor_copy(out=y_sb[:], in_=y[:])
+                nc.vector.scalar_tensor_tensor(out=size[:], in0=y_sb[:], scalar=-1.0, in1=y_sb[:], op0=ALU.mult, op1=ALU.max)
+            vol = keep.tile([P, COLS], F32, name=f"vol{i}")
+            nc.scalar.activation(out=vol[:], in_=size[:], func=ACT.Sqrt, bias=spec_sb[:, c : c + 1])
+            nc.sync.dma_start(out=out[c * P : (c + 1) * P, h * COLS : (h + 1) * COLS], in_=vol[:])

@@ -1,6 +1,7 @@
 from contextlib import ExitStack
 
 import concourse.mybir as mybir
+from concourse.masks import make_identity
 
 K, T, S, H, N = 1536, 2048, 1024, 512, 1536
 FLOPS = 2 * K * H * S + 2 * H * N * S
@@ -23,8 +24,7 @@ COLS = 512
 HALVES = S // COLS
 N_TILES = N // P
 CHUNK = 256
-MOVED_ROWS = 100
-FIRST_ROW = 32 - 4 * PASSES
+MOVED_ROWS = 112
 
 
 def tile_list_shock_factor_vols_kernel(tc, tab_words, tab_scales, offs, w1, gain, w4_words, w4_scales, spec, out):
@@ -32,86 +32,72 @@ def tile_list_shock_factor_vols_kernel(tc, tab_words, tab_scales, offs, w1, gain
     with ExitStack() as ctx:
         keep = ctx.enter_context(tc.tile_pool(name="keep", bufs=1))
         ring = ctx.enter_context(tc.tile_pool(name="ring", bufs=4))
+        stage = ctx.enter_context(tc.tile_pool(name="stage", bufs=4))
+        shared = ctx.enter_context(tc.tile_pool(name="shared", bufs=1))
         psum = ctx.enter_context(tc.psum_pool(name="psum", bufs=1))
 
         offsets = keep.tile([P, S // 16], U16, name="offsets")
         nc.sync.dma_start(offsets[:], offs)
 
-        tab_plane = keep.tile([P, T], U8, name="tab_plane", align_bytes=64)
-        for q in range(4):
-            nc.vector.memset(tab_plane[32 * q : 32 * q + FIRST_ROW, :].bitcast(I32), 0)
-        picked = keep.tile([P, S], U8, name="picked", align_bytes=64)
-        v_planes = [keep.tile([P, S], U8, name=f"v_plane{a}", align_bytes=64) for a in range(PASSES)]
-        for a in range(PASSES):
-            nc.vector.memset(v_planes[a][:].bitcast(I32), 0)
-        w4_plane = keep.tile([P, N], U8, name="w4_plane", align_bytes=64)
-        nc.vector.memset(w4_plane[:].bitcast(I32), 0)
+        warm = keep.tile([P, 1], F32, name="warm")
+        nc.gpsimd.memset(warm[:], 1.0)
+        tab_plane = shared.tile([P, T], U8, name="tab_plane", align_bytes=64, offset=4 * S + H - T)
+        nc.gpsimd.memset(tab_plane[:].bitcast(I32), 0)
 
-        tabs = [keep.tile([P, T], I32, name=f"tab{a}", align_bytes=64) for a in range(PASSES)]
-        raws = [keep.tile([P, PACK, H], F32, name=f"w1_raw{a}", align_bytes=64) for a in range(PASSES)]
-
-        def load_tab(a, queue):
-            queue.dma_start(out=tabs[a][:], in_=tab_words[a].rearrange("p t i -> p (t i)").bitcast(I32))
+        def load_tab(a):
+            tab = stage.tile([P, T], I32, name=f"tab{a}", tag="stage", align_bytes=64)
+            nc.scalar.dma_start(out=tab[:], in_=tab_words[a].rearrange("p t i -> p (t i)").bitcast(I32))
+            return tab
 
         def load_w1(a):
+            raw = stage.tile([P, PACK, H], F32, name=f"w1_raw{a}", tag="stage", align_bytes=64)
             rows = w1[a * P * PACK : (a + 1) * P * PACK, :]
-            nc.sync.dma_start(out=raws[a][:], in_=rows.rearrange("(p j) c -> p j c", j=PACK))
+            nc.scalar.dma_start(out=raw[:], in_=rows.rearrange("(p j) c -> p j c", j=PACK))
+            return raw
 
-        load_tab(0, nc.scalar)
-        load_tab(1, nc.scalar)
+        tabs = [load_tab(0)]
+        warm_out = keep.tile([P, 1], F32, name="warm_out")
+        nc.scalar.activation(out=warm_out[:], in_=warm[:], func=ACT.Sqrt)
+        raws = [load_w1(0)]
+        tabs.append(load_tab(1))
+        raws.append(load_w1(1))
         for q in range(4):
             nc.sync.dma_start(
-                out=tab_plane[32 * q + FIRST_ROW : 32 * q + 32, :].bitcast(I32),
+                out=tab_plane[32 * q : 32 * q + 4 * PASSES, :].bitcast(I32),
                 in_=tab_scales[:, 4 * q : 4 * q + 4, :].bitcast(I32),
             )
-        load_w1(0)
-        load_w1(1)
-        load_w1(2)
-        load_tab(2, nc.sync)
-        warm = keep.tile([P, 1], F32, name="warm")
-        warm_out = keep.tile([P, 1], F32, name="warm_out")
-        nc.vector.memset(warm[:], 1.0)
-        nc.scalar.activation(out=warm_out[:], in_=warm[:], func=ACT.Sqrt)
+
+        v_planes = [keep.tile([P, S], U8, name=f"v_plane{a}", tag=f"plane{a}", align_bytes=64) for a in range(PASSES)]
+        for a in range(1, PASSES):
+            nc.vector.memset(v_planes[a][:].bitcast(I32), 0)
 
         gain_sb = keep.tile([P, PACK], F32, name="gain_sb")
-        nc.sync.dma_start(out=gain_sb[:], in_=gain.rearrange("(p t) -> p t", t=PACK))
-        w4_codes = keep.tile([P, N], I32, name="w4_codes", align_bytes=64)
-        nc.sync.dma_start(out=w4_codes[:], in_=w4_words[0].rearrange("p c i -> p (c i)").bitcast(I32))
+        nc.gpsimd.dma_start(out=gain_sb[:], in_=gain.rearrange("(p t) -> p t", t=PACK))
+        spec_rows = keep.tile([P, P], F32, name="spec_rows")
+        nc.vector.memset(spec_rows[:], 0.0)
+        nc.gpsimd.dma_start(out=spec_rows[0:N_TILES, :], in_=spec.rearrange("(c p) -> c p", p=P))
+        identity = keep.tile([P, P], F32, name="identity")
+        make_identity(nc, identity[:])
+        spec_bank = psum.tile([P, P], F32, name="spec_bank", tag="bank7")
+        nc.tensor.transpose(spec_bank[:], spec_rows[:], identity[:])
         spec_sb = keep.tile([P, N_TILES], F32, name="spec_sb")
-        with nc.allow_non_contiguous_dma(reason="one value of spec for each partition and tile of rows"):
-            nc.sync.dma_start(out=spec_sb[:], in_=spec.rearrange("(c p) -> p c", p=P))
-        for q in range(4):
-            nc.sync.dma_start(
-                out=w4_plane[32 * q : 32 * q + 4, :].bitcast(I32),
-                in_=w4_scales[0, 4 * q : 4 * q + 4, :].bitcast(I32),
-            )
+        nc.scalar.copy(out=spec_sb[:], in_=spec_bank[:, 0:N_TILES])
 
-        v_codes = [[keep.tile([P, COLS], U32, name=f"v_codes{a}_{h}", align_bytes=64) for h in range(HALVES)] for a in range(PASSES)]
         grouped = [keep.tile([P, H * PACK], BF16, name=f"w1_grouped{a}", align_bytes=64) for a in range(PASSES)]
         w1_codes = [keep.tile([P, H], U32, name=f"w1_codes{a}", align_bytes=64) for a in range(PASSES)]
-        w1_planes = [keep.tile([P, H], U8, name=f"w1_plane{a}", align_bytes=64) for a in range(PASSES)]
         f_banks = [[psum.tile([P, COLS], F32, name=f"f{h}_{t}", tag=f"bank{PACK * h + t}") for t in range(PACK)] for h in range(HALVES)]
 
-        def gather_words(a, h):
-            cols = COLS // 16
-            nc.vector.tensor_copy(out=v_codes[a][h][:], in_=tabs[a][:].bitcast(U32).indirect(offsets[:, h * cols : (h + 1) * cols]))
+        def gather_words(a, codes, j0, j1):
+            nc.vector.tensor_copy(out=codes[:, j0:j1], in_=tabs[a][:].bitcast(U32).indirect(offsets[:, j0 // 16 : j1 // 16]))
 
-        def gather_scales():
-            nc.vector.tensor_copy(out=picked[:], in_=tab_plane[:].indirect(offsets[:]))
-            for a in range(PASSES):
-                nc.gpsimd.dma_start(
-                    out=v_planes[a][0:MOVED_ROWS, :].bitcast(I32),
-                    in_=picked[FIRST_ROW + 4 * a : FIRST_ROW + 4 * a + MOVED_ROWS, :].bitcast(I32),
-                )
-
-        def cast_w1(a, copy):
+        def cast_w1(a, copy, m0, m1):
             copy(
-                out=grouped[a][:].rearrange("p (t m j) -> p m j t", t=PACK, j=PACK),
-                in_=raws[a][:].rearrange("p j (m t) -> p m j t", t=PACK),
+                out=grouped[a][:].rearrange("p (t m j) -> p m j t", t=PACK, j=PACK)[:, m0:m1],
+                in_=raws[a][:].rearrange("p j (m t) -> p m j t", t=PACK)[:, m0:m1],
             )
 
-        def quantize_w1(a):
-            nc.vector.quantize_mx(out=w1_codes[a][:].bitcast(E4M3), scales=w1_planes[a][:], in_=grouped[a][:])
+        def quantize_w1(a, plane):
+            nc.vector.quantize_mx(out=w1_codes[a][:].bitcast(E4M3), scales=plane[:], in_=grouped[a][:])
 
         def first_product(a, h):
             for t in range(PACK):
@@ -119,29 +105,49 @@ def tile_list_shock_factor_vols_kernel(tc, tab_words, tab_scales, offs, w1, gain
                     out=f_banks[h][t][:],
                     lhsT=w1_codes[a][:, t * P : (t + 1) * P].bitcast(E4M3),
                     lhsT_scale=w1_planes[a][:, t * P : (t + 1) * P],
-                    rhs=v_codes[a][h][:].bitcast(E5M2),
+                    rhs=v_codes[a][:, h * COLS : (h + 1) * COLS].bitcast(E5M2),
                     rhs_scale=v_planes[a][:, h * COLS : (h + 1) * COLS],
                     start=(a == 0),
                     stop=(a == PASSES - 1),
                 )
 
-        gather_words(0, 0)
-        gather_words(0, 1)
-        gather_scales()
-        gather_words(1, 0)
-        gather_words(1, 1)
-        cast_w1(0, nc.scalar.copy)
-        quantize_w1(0)
+        v_codes = [keep.tile([P, S], U32, name="v_codes0", align_bytes=64)]
+        gather_words(0, v_codes[0], 0, S)
+        raws.append(load_w1(2))
+        nc.vector.tensor_copy(out=v_planes[0][:], in_=tab_plane[:].indirect(offsets[:]))
+        for a in range(1, PASSES):
+            nc.sync.dma_start(
+                out=v_planes[a][0:MOVED_ROWS, :].bitcast(I32),
+                in_=v_planes[0][4 * a : 4 * a + MOVED_ROWS, :].bitcast(I32),
+            )
+        cast_w1(0, nc.scalar.copy, 0, P)
+        tabs.append(load_tab(2))
+        v_codes.append(shared.tile([P, S], U32, name="v_codes1", align_bytes=64, offset=0))
+        v_codes.append(keep.tile([P, S], U32, name="v_codes2", align_bytes=64))
+        w1_planes = [shared.tile([P, H], U8, name="w1_plane0", align_bytes=64, offset=4 * S)]
+        w1_planes.extend(keep.tile([P, H], U8, name=f"w1_plane{a}", align_bytes=64) for a in range(1, PASSES))
+        gather_words(1, v_codes[1], 0, S)
+        w4_codes = stage.tile([P, N], I32, name="w4_codes", tag="stage", align_bytes=64)
+        nc.scalar.dma_start(out=w4_codes[:], in_=w4_words[0].rearrange("p c i -> p (c i)").bitcast(I32))
+        quantize_w1(0, w1_planes[0])
         first_product(0, 0)
         first_product(0, 1)
-        cast_w1(1, nc.scalar.copy)
-        cast_w1(2, nc.vector.tensor_copy)
-        quantize_w1(1)
+        w4_plane = keep.tile([P, N], U8, name="w4_plane", tag="plane0", align_bytes=64)
+        nc.gpsimd.memset(w4_plane[:].bitcast(I32), 0)
+        for q in range(4):
+            nc.sync.dma_start(
+                out=w4_plane[32 * q : 32 * q + 4, :].bitcast(I32),
+                in_=w4_scales[0, 4 * q : 4 * q + 4, :].bitcast(I32),
+            )
+        cast_w1(1, nc.scalar.copy, 0, P)
+        quantize_w1(1, w1_planes[1])
         first_product(1, 0)
         first_product(1, 1)
-        quantize_w1(2)
+        cast_w1(2, nc.vector.tensor_copy, 0, P // 2)
+        cast_w1(2, nc.scalar.copy, P // 2, P)
+        quantize_w1(2, w1_planes[2])
         for h in range(HALVES):
-            gather_words(2, h)
+            gather_words(2, v_codes[2], h * COLS, (h + 1) * COLS)
             first_product(2, h)
 
         squares = [keep.tile([P, PACK, COLS], F32, name=f"squares{h}", align_bytes=64) for h in range(HALVES)]
@@ -185,9 +191,9 @@ def tile_list_shock_factor_vols_kernel(tc, tab_words, tab_scales, offs, w1, gain
             if i < 3 or i % 3 == 2:
                 nc.scalar.activation(out=size[:], in_=y[:], func=ACT.Abs)
             else:
-                y_sb = ring.tile([P, COLS], F32, name="y_sb")
-                nc.vector.tensor_copy(out=y_sb[:], in_=y[:])
-                nc.vector.scalar_tensor_tensor(out=size[:], in0=y_sb[:], scalar=-1.0, in1=y_sb[:], op0=ALU.mult, op1=ALU.max)
+                minus_y = ring.tile([P, COLS], F32, name="minus_y")
+                nc.vector.tensor_scalar_mul(out=minus_y[:], in0=y[:], scalar1=-1.0)
+                nc.vector.tensor_tensor(out=size[:], in0=y[:], in1=minus_y[:], op=ALU.max)
             vol = keep.tile([P, COLS], F32, name=f"vol{i}")
             nc.scalar.activation(out=vol[:], in_=size[:], func=ACT.Sqrt, bias=spec_sb[:, c : c + 1])
             nc.sync.dma_start(out=out[c * P : (c + 1) * P, h * COLS : (h + 1) * COLS], in_=vol[:])

@@ -24,7 +24,9 @@ COLS = 512
 HALVES = S // COLS
 N_TILES = N // P
 CHUNK = 256
-MOVED_ROWS = 112
+MOVED_ROWS = 100
+FIRST_ROW = 32 - 4 * PASSES
+STAGE_BYTES = 4 * T
 
 
 def tile_list_shock_factor_vols_kernel(tc, tab_words, tab_scales, offs, w1, gain, w4_words, w4_scales, spec, out):
@@ -32,7 +34,6 @@ def tile_list_shock_factor_vols_kernel(tc, tab_words, tab_scales, offs, w1, gain
     with ExitStack() as ctx:
         keep = ctx.enter_context(tc.tile_pool(name="keep", bufs=1))
         ring = ctx.enter_context(tc.tile_pool(name="ring", bufs=4))
-        stage = ctx.enter_context(tc.tile_pool(name="stage", bufs=4))
         shared = ctx.enter_context(tc.tile_pool(name="shared", bufs=1))
         psum = ctx.enter_context(tc.psum_pool(name="psum", bufs=1))
 
@@ -41,41 +42,39 @@ def tile_list_shock_factor_vols_kernel(tc, tab_words, tab_scales, offs, w1, gain
 
         warm = keep.tile([P, 1], F32, name="warm")
         nc.gpsimd.memset(warm[:], 1.0)
-        tab_plane = shared.tile([P, T], U8, name="tab_plane", align_bytes=64, offset=4 * S + H - T)
-        nc.gpsimd.memset(tab_plane[:].bitcast(I32), 0)
-
-        def load_tab(a):
-            tab = stage.tile([P, T], I32, name=f"tab{a}", tag="stage", align_bytes=64)
-            nc.scalar.dma_start(out=tab[:], in_=tab_words[a].rearrange("p t i -> p (t i)").bitcast(I32))
-            return tab
-
-        def load_w1(a):
-            raw = stage.tile([P, PACK, H], F32, name=f"w1_raw{a}", tag="stage", align_bytes=64)
-            rows = w1[a * P * PACK : (a + 1) * P * PACK, :]
-            nc.scalar.dma_start(out=raw[:], in_=rows.rearrange("(p j) c -> p j c", j=PACK))
-            return raw
-
-        tabs = [load_tab(0)]
-        warm_out = keep.tile([P, 1], F32, name="warm_out")
-        nc.scalar.activation(out=warm_out[:], in_=warm[:], func=ACT.Sqrt)
-        raws = [load_w1(0)]
-        tabs.append(load_tab(1))
-        raws.append(load_w1(1))
+        spec_rows = keep.tile([P, P], F32, name="spec_rows")
+        nc.gpsimd.memset(spec_rows[:], 0.0)
+        nc.gpsimd.dma_start(out=spec_rows[0:N_TILES, :], in_=spec.rearrange("(c p) -> c p", p=P))
+        tab_plane = shared.tile([P, T], U8, name="tab_plane", align_bytes=64, offset=STAGE_BYTES - (T - N) // 2)
         for q in range(4):
             nc.sync.dma_start(
-                out=tab_plane[32 * q : 32 * q + 4 * PASSES, :].bitcast(I32),
+                out=tab_plane[32 * q + FIRST_ROW : 32 * q + 32, :].bitcast(I32),
                 in_=tab_scales[:, 4 * q : 4 * q + 4, :].bitcast(I32),
             )
+            nc.vector.memset(tab_plane[32 * q : 32 * q + FIRST_ROW, :].bitcast(I32), 0)
 
-        v_planes = [keep.tile([P, S], U8, name=f"v_plane{a}", tag=f"plane{a}", align_bytes=64) for a in range(PASSES)]
-        for a in range(1, PASSES):
+        def load_tab(a, tab):
+            nc.sync.dma_start(out=tab[:], in_=tab_words[a].rearrange("p t i -> p (t i)").bitcast(I32))
+            return tab
+
+        def load_w1(a, raw, queue):
+            rows = w1[a * P * PACK : (a + 1) * P * PACK, :]
+            queue.dma_start(out=raw[:], in_=rows.rearrange("(p j) c -> p j c", j=PACK))
+            return raw
+
+        raws = [load_w1(0, keep.tile([P, PACK, H], F32, name="w1_raw0"), nc.scalar)]
+        warm_out = keep.tile([P, 1], F32, name="warm_out")
+        nc.scalar.activation(out=warm_out[:], in_=warm[:], func=ACT.Sqrt)
+        tabs = [load_tab(0, keep.tile([P, T], I32, name="tab0", align_bytes=64))]
+        raws.append(load_w1(1, keep.tile([P, PACK, H], F32, name="w1_raw1", tag="w1_raw1", align_bytes=64), nc.sync))
+        tabs.append(load_tab(1, keep.tile([P, T], I32, name="tab1", align_bytes=64)))
+
+        v_planes = [keep.tile([P, S], U8, name=f"v_plane{a}", align_bytes=64) for a in range(PASSES)]
+        for a in range(PASSES):
             nc.vector.memset(v_planes[a][:].bitcast(I32), 0)
 
         gain_sb = keep.tile([P, PACK], F32, name="gain_sb")
         nc.gpsimd.dma_start(out=gain_sb[:], in_=gain.rearrange("(p t) -> p t", t=PACK))
-        spec_rows = keep.tile([P, P], F32, name="spec_rows")
-        nc.vector.memset(spec_rows[:], 0.0)
-        nc.gpsimd.dma_start(out=spec_rows[0:N_TILES, :], in_=spec.rearrange("(c p) -> c p", p=P))
         identity = keep.tile([P, P], F32, name="identity")
         make_identity(nc, identity[:])
         spec_bank = psum.tile([P, P], F32, name="spec_bank", tag="bank7")
@@ -90,10 +89,10 @@ def tile_list_shock_factor_vols_kernel(tc, tab_words, tab_scales, offs, w1, gain
         def gather_words(a, codes, j0, j1):
             nc.vector.tensor_copy(out=codes[:, j0:j1], in_=tabs[a][:].bitcast(U32).indirect(offsets[:, j0 // 16 : j1 // 16]))
 
-        def cast_w1(a, copy, m0, m1):
+        def cast_w1(a, u, copy):
             copy(
-                out=grouped[a][:].rearrange("p (t m j) -> p m j t", t=PACK, j=PACK)[:, m0:m1],
-                in_=raws[a][:].rearrange("p j (m t) -> p m j t", t=PACK)[:, m0:m1],
+                out=grouped[a][:].rearrange("p (u e m j) -> p u m e j", u=2, e=2, j=PACK)[:, u],
+                in_=raws[a][:].rearrange("p j (m u e) -> p u m e j", u=2, e=2)[:, u],
             )
 
         def quantize_w1(a, plane):
@@ -111,40 +110,36 @@ def tile_list_shock_factor_vols_kernel(tc, tab_words, tab_scales, offs, w1, gain
                     stop=(a == PASSES - 1),
                 )
 
-        v_codes = [keep.tile([P, S], U32, name="v_codes0", align_bytes=64)]
-        gather_words(0, v_codes[0], 0, S)
-        raws.append(load_w1(2))
-        nc.vector.tensor_copy(out=v_planes[0][:], in_=tab_plane[:].indirect(offsets[:]))
-        for a in range(1, PASSES):
+        picked = keep.tile([P, S], U8, name="picked", align_bytes=64)
+        nc.vector.tensor_copy(out=picked[:], in_=tab_plane[:].indirect(offsets[:]))
+        for a in range(PASSES):
             nc.sync.dma_start(
                 out=v_planes[a][0:MOVED_ROWS, :].bitcast(I32),
-                in_=v_planes[0][4 * a : 4 * a + MOVED_ROWS, :].bitcast(I32),
+                in_=picked[FIRST_ROW + 4 * a : FIRST_ROW + 4 * a + MOVED_ROWS, :].bitcast(I32),
             )
-        cast_w1(0, nc.scalar.copy, 0, P)
-        tabs.append(load_tab(2))
-        v_codes.append(shared.tile([P, S], U32, name="v_codes1", align_bytes=64, offset=0))
-        v_codes.append(keep.tile([P, S], U32, name="v_codes2", align_bytes=64))
-        w1_planes = [shared.tile([P, H], U8, name="w1_plane0", align_bytes=64, offset=4 * S)]
-        w1_planes.extend(keep.tile([P, H], U8, name=f"w1_plane{a}", align_bytes=64) for a in range(1, PASSES))
-        gather_words(1, v_codes[1], 0, S)
-        w4_codes = stage.tile([P, N], I32, name="w4_codes", tag="stage", align_bytes=64)
-        nc.scalar.dma_start(out=w4_codes[:], in_=w4_words[0].rearrange("p c i -> p (c i)").bitcast(I32))
-        quantize_w1(0, w1_planes[0])
-        first_product(0, 0)
-        first_product(0, 1)
-        w4_plane = keep.tile([P, N], U8, name="w4_plane", tag="plane0", align_bytes=64)
+        raws.append(load_w1(2, shared.tile([P, PACK, H], F32, name="w1_raw2", align_bytes=64, offset=0), nc.sync))
+        tabs.append(load_tab(2, shared.tile([P, T], I32, name="tab2", align_bytes=64, offset=STAGE_BYTES + N)))
+        w4_plane = shared.tile([P, N], U8, name="w4_plane", align_bytes=64, offset=STAGE_BYTES)
         nc.gpsimd.memset(w4_plane[:].bitcast(I32), 0)
         for q in range(4):
             nc.sync.dma_start(
                 out=w4_plane[32 * q : 32 * q + 4, :].bitcast(I32),
                 in_=w4_scales[0, 4 * q : 4 * q + 4, :].bitcast(I32),
             )
-        cast_w1(1, nc.scalar.copy, 0, P)
-        quantize_w1(1, w1_planes[1])
-        first_product(1, 0)
-        first_product(1, 1)
-        cast_w1(2, nc.vector.tensor_copy, 0, P // 2)
-        cast_w1(2, nc.scalar.copy, P // 2, P)
+
+        v_codes = [keep.tile([P, S], U32, name=f"v_codes{a}", align_bytes=64) for a in range(PASSES)]
+        w1_planes = [keep.tile([P, H], U8, name=f"w1_plane{a}", align_bytes=64) for a in range(PASSES)]
+        for a in range(PASSES - 1):
+            cast_w1(a, 0, nc.scalar.copy)
+            cast_w1(a, 1, nc.scalar.copy)
+            gather_words(a, v_codes[a], 0, S)
+            quantize_w1(a, w1_planes[a])
+            first_product(a, 0)
+            first_product(a, 1)
+        w4_codes = keep.tile([P, N], I32, name="w4_codes", tag="w1_raw1", align_bytes=64)
+        nc.sync.dma_start(out=w4_codes[:], in_=w4_words[0].rearrange("p c i -> p (c i)").bitcast(I32))
+        cast_w1(2, 0, nc.vector.tensor_copy)
+        cast_w1(2, 1, nc.scalar.copy)
         quantize_w1(2, w1_planes[2])
         for h in range(HALVES):
             gather_words(2, v_codes[2], h * COLS, (h + 1) * COLS)
@@ -154,25 +149,25 @@ def tile_list_shock_factor_vols_kernel(tc, tab_words, tab_scales, offs, w1, gain
         h_grouped = [keep.tile([P, COLS * PACK], BF16, name=f"h_grouped{h}", align_bytes=64) for h in range(HALVES)]
         h_codes = [keep.tile([P, COLS], U32, name=f"h_codes{h}", align_bytes=64) for h in range(HALVES)]
         h_planes = [keep.tile([P, COLS], U8, name=f"h_plane{h}", align_bytes=64) for h in range(HALVES)]
-        gain_rows = gain_sb[:].unsqueeze(1).unsqueeze(3).to_broadcast([P, CHUNK // 4, PACK, 4])
+        h_rows = [keep.tile([P, PACK, COLS], BF16, name=f"h_rows{h}", align_bytes=64) for h in range(HALVES)]
 
         for h, width in enumerate((CHUNK, COLS)):
             for c0 in range(0, COLS, width):
                 for t in range(PACK):
                     nc.scalar.activation(out=squares[h][:, t, c0 : c0 + width], in_=f_banks[h][t][:, c0 : c0 + width], func=ACT.Square)
-        for h in range(HALVES):
-            for c0 in range(0, COLS, CHUNK):
-                nc.vector.tensor_tensor(
-                    out=h_grouped[h][:, c0 * PACK : (c0 + CHUNK) * PACK].rearrange("p (c i t) -> p c t i", i=4, t=PACK),
-                    in0=squares[h][:, :, c0 : c0 + CHUNK].rearrange("p t (c i) -> p c t i", i=4),
-                    in1=gain_rows,
-                    op=ALU.mult,
+        for h, width in enumerate((CHUNK, COLS)):
+            for c0 in range(0, COLS, width):
+                for t in range(PACK):
+                    nc.vector.tensor_scalar_mul(out=h_rows[h][:, t, c0 : c0 + width], in0=squares[h][:, t, c0 : c0 + width], scalar1=gain_sb[:, t : t + 1])
+                nc.vector.tensor_copy(
+                    out=h_grouped[h][:, c0 * PACK : (c0 + width) * PACK].rearrange("p (c t) -> p c t", t=PACK),
+                    in_=h_rows[h][:, :, c0 : c0 + width].rearrange("p t c -> p c t"),
                 )
-            for c0 in range(0, COLS, CHUNK):
+            for c0 in range(0, COLS, width):
                 nc.vector.quantize_mx(
-                    out=h_codes[h][:, c0 : c0 + CHUNK].bitcast(E4M3),
-                    scales=h_planes[h][:, c0 : c0 + CHUNK],
-                    in_=h_grouped[h][:, c0 * PACK : (c0 + CHUNK) * PACK],
+                    out=h_codes[h][:, c0 : c0 + width].bitcast(E4M3),
+                    scales=h_planes[h][:, c0 : c0 + width],
+                    in_=h_grouped[h][:, c0 * PACK : (c0 + width) * PACK],
                 )
 
         for i in range(HALVES * N_TILES):

@@ -33,7 +33,7 @@ def tile_list_shock_factor_vols_kernel(tc, tab_words, tab_scales, offs, w1, gain
     nc = tc.nc
     with ExitStack() as ctx:
         keep = ctx.enter_context(tc.tile_pool(name="keep", bufs=1))
-        ring = ctx.enter_context(tc.tile_pool(name="ring", bufs=4))
+        ring = ctx.enter_context(tc.tile_pool(name="ring", bufs=6))
         shared = ctx.enter_context(tc.tile_pool(name="shared", bufs=1))
         psum = ctx.enter_context(tc.psum_pool(name="psum", bufs=1))
 
@@ -42,15 +42,13 @@ def tile_list_shock_factor_vols_kernel(tc, tab_words, tab_scales, offs, w1, gain
 
         warm = keep.tile([P, 1], F32, name="warm")
         nc.gpsimd.memset(warm[:], 1.0)
+        identity = keep.tile([P, P], F32, name="identity")
+        make_identity(nc, identity[:])
         spec_rows = keep.tile([P, P], F32, name="spec_rows")
         nc.gpsimd.memset(spec_rows[:], 0.0)
         nc.gpsimd.dma_start(out=spec_rows[0:N_TILES, :], in_=spec.rearrange("(c p) -> c p", p=P))
         tab_plane = shared.tile([P, T], U8, name="tab_plane", align_bytes=64, offset=STAGE_BYTES - (T - N) // 2)
         for q in range(4):
-            nc.sync.dma_start(
-                out=tab_plane[32 * q + FIRST_ROW : 32 * q + 32, :].bitcast(I32),
-                in_=tab_scales[:, 4 * q : 4 * q + 4, :].bitcast(I32),
-            )
             nc.vector.memset(tab_plane[32 * q : 32 * q + FIRST_ROW, :].bitcast(I32), 0)
 
         def load_tab(a, tab):
@@ -63,6 +61,11 @@ def tile_list_shock_factor_vols_kernel(tc, tab_words, tab_scales, offs, w1, gain
             return raw
 
         raws = [load_w1(0, keep.tile([P, PACK, H], F32, name="w1_raw0"), nc.scalar)]
+        for q, queue in enumerate((nc.sync, nc.sync, nc.sync, nc.scalar)):
+            queue.dma_start(
+                out=tab_plane[32 * q + FIRST_ROW : 32 * q + 32, :].bitcast(I32),
+                in_=tab_scales[:, 4 * q : 4 * q + 4, :].bitcast(I32),
+            )
         warm_out = keep.tile([P, 1], F32, name="warm_out")
         nc.scalar.activation(out=warm_out[:], in_=warm[:], func=ACT.Sqrt)
         tabs = [load_tab(0, keep.tile([P, T], I32, name="tab0", align_bytes=64))]
@@ -74,9 +77,7 @@ def tile_list_shock_factor_vols_kernel(tc, tab_words, tab_scales, offs, w1, gain
             nc.vector.memset(v_planes[a][:].bitcast(I32), 0)
 
         gain_sb = keep.tile([P, PACK], F32, name="gain_sb")
-        nc.gpsimd.dma_start(out=gain_sb[:], in_=gain.rearrange("(p t) -> p t", t=PACK))
-        identity = keep.tile([P, P], F32, name="identity")
-        make_identity(nc, identity[:])
+        nc.scalar.dma_start(out=gain_sb[:], in_=gain.rearrange("(p t) -> p t", t=PACK))
         spec_bank = psum.tile([P, P], F32, name="spec_bank", tag="bank7")
         nc.tensor.transpose(spec_bank[:], spec_rows[:], identity[:])
         spec_sb = keep.tile([P, N_TILES], F32, name="spec_sb")
@@ -112,12 +113,17 @@ def tile_list_shock_factor_vols_kernel(tc, tab_words, tab_scales, offs, w1, gain
 
         picked = keep.tile([P, S], U8, name="picked", align_bytes=64)
         nc.vector.tensor_copy(out=picked[:], in_=tab_plane[:].indirect(offsets[:]))
-        for a in range(PASSES):
+
+        def move_plane(a):
             nc.sync.dma_start(
                 out=v_planes[a][0:MOVED_ROWS, :].bitcast(I32),
                 in_=picked[FIRST_ROW + 4 * a : FIRST_ROW + 4 * a + MOVED_ROWS, :].bitcast(I32),
             )
+
+        move_plane(0)
         raws.append(load_w1(2, shared.tile([P, PACK, H], F32, name="w1_raw2", align_bytes=64, offset=0), nc.sync))
+        move_plane(1)
+        move_plane(2)
         tabs.append(load_tab(2, shared.tile([P, T], I32, name="tab2", align_bytes=64, offset=STAGE_BYTES + N)))
         w4_plane = shared.tile([P, N], U8, name="w4_plane", align_bytes=64, offset=STAGE_BYTES)
         nc.gpsimd.memset(w4_plane[:].bitcast(I32), 0)
@@ -146,49 +152,101 @@ def tile_list_shock_factor_vols_kernel(tc, tab_words, tab_scales, offs, w1, gain
             first_product(2, h)
 
         squares = [keep.tile([P, PACK, COLS], F32, name=f"squares{h}", align_bytes=64) for h in range(HALVES)]
-        h_grouped = [keep.tile([P, COLS * PACK], BF16, name=f"h_grouped{h}", align_bytes=64) for h in range(HALVES)]
+        h_grouped = [keep.tile([P, COLS * PACK], BF16, name=f"h_grouped{h}", tag=f"h_grouped{h}", align_bytes=64) for h in range(HALVES)]
         h_codes = [keep.tile([P, COLS], U32, name=f"h_codes{h}", align_bytes=64) for h in range(HALVES)]
         h_planes = [keep.tile([P, COLS], U8, name=f"h_plane{h}", align_bytes=64) for h in range(HALVES)]
-        h_rows = [keep.tile([P, PACK, COLS], BF16, name=f"h_rows{h}", align_bytes=64) for h in range(HALVES)]
+        h_rows = [keep.tile([P, PACK, COLS], BF16, name="h_rows0", align_bytes=64)]
 
         for h, width in enumerate((CHUNK, COLS)):
             for c0 in range(0, COLS, width):
                 for t in range(PACK):
                     nc.scalar.activation(out=squares[h][:, t, c0 : c0 + width], in_=f_banks[h][t][:, c0 : c0 + width], func=ACT.Square)
-        for h, width in enumerate((CHUNK, COLS)):
-            for c0 in range(0, COLS, width):
-                for t in range(PACK):
-                    nc.vector.tensor_scalar_mul(out=h_rows[h][:, t, c0 : c0 + width], in0=squares[h][:, t, c0 : c0 + width], scalar1=gain_sb[:, t : t + 1])
-                nc.vector.tensor_copy(
-                    out=h_grouped[h][:, c0 * PACK : (c0 + width) * PACK].rearrange("p (c t) -> p c t", t=PACK),
-                    in_=h_rows[h][:, :, c0 : c0 + width].rearrange("p t c -> p c t"),
-                )
-            for c0 in range(0, COLS, width):
-                nc.vector.quantize_mx(
-                    out=h_codes[h][:, c0 : c0 + width].bitcast(E4M3),
-                    scales=h_planes[h][:, c0 : c0 + width],
-                    in_=h_grouped[h][:, c0 * PACK : (c0 + width) * PACK],
+
+        def weigh(h, cols, engine):
+            for t in range(PACK):
+                engine.tensor_scalar(
+                    out=h_rows[h][:, t, cols], in0=squares[h][:, t, cols],
+                    scalar1=gain_sb[:, t : t + 1], scalar2=0.0, op0=ALU.mult, op1=ALU.add,
                 )
 
-        for i in range(HALVES * N_TILES):
+        def interleave(h, cols):
+            nc.vector.tensor_copy(
+                out=h_grouped[h][:].rearrange("p (c t) -> p c t", t=PACK)[:, cols],
+                in_=h_rows[h][:].rearrange("p t c -> p c t")[:, cols],
+            )
+
+        def quantize_h(h, cols):
+            nc.vector.quantize_mx(
+                out=h_codes[h][:, cols].bitcast(E4M3),
+                scales=h_planes[h][:, cols],
+                in_=h_grouped[h][:, cols.start * PACK : cols.stop * PACK],
+            )
+
+        first, second, whole = slice(0, CHUNK), slice(CHUNK, COLS), slice(0, COLS)
+        weigh(0, first, nc.vector)
+        interleave(0, first)
+        weigh(0, second, nc.vector)
+        quantize_h(0, first)
+        interleave(0, second)
+        quantize_h(0, second)
+        h_rows.append(keep.tile([P, PACK, COLS], BF16, name="h_rows1", tag="h_grouped0", align_bytes=64))
+        weigh(1, whole, nc.gpsimd)
+
+        def second_product(i, y, cols):
             h, c = divmod(i, N_TILES)
-            y = psum.tile([P, COLS], F32, name=f"y{i}", tag=f"bank{i % 8}")
             nc.tensor.matmul_mx(
-                out=y[:],
+                out=y[:, cols],
                 lhsT=w4_codes[:, c * P : (c + 1) * P].bitcast(E4M3),
                 lhsT_scale=w4_plane[:, c * P : (c + 1) * P],
-                rhs=h_codes[h][:].bitcast(E4M3),
-                rhs_scale=h_planes[h][:],
+                rhs=h_codes[h][:, cols].bitcast(E4M3),
+                rhs_scale=h_planes[h][:, cols],
                 start=True,
                 stop=True,
             )
+
+        def new_bank(i):
+            return psum.tile([P, COLS], F32, name=f"y{i}", tag=f"bank{i % 8}")
+
+        def abs_on_scalar(y, size, cols):
+            nc.scalar.activation(out=size[:, cols], in_=y[:, cols], func=ACT.Abs)
+
+        def negate(y):
+            minus_y = ring.tile([P, COLS], F32, name="minus_y")
+            nc.vector.tensor_scalar_mul(out=minus_y[:], in0=y[:], scalar1=-1.0)
+            return minus_y
+
+        def larger(y, minus_y):
             size = ring.tile([P, COLS], F32, name="size")
-            if i < 3 or i % 3 == 2:
-                nc.scalar.activation(out=size[:], in_=y[:], func=ACT.Abs)
-            else:
-                minus_y = ring.tile([P, COLS], F32, name="minus_y")
-                nc.vector.tensor_scalar_mul(out=minus_y[:], in0=y[:], scalar1=-1.0)
-                nc.vector.tensor_tensor(out=size[:], in0=y[:], in1=minus_y[:], op=ALU.max)
+            nc.vector.tensor_tensor(out=size[:], in0=y[:], in1=minus_y[:], op=ALU.max)
+            return size
+
+        def finish(i, size):
+            h, c = divmod(i, N_TILES)
             vol = keep.tile([P, COLS], F32, name=f"vol{i}")
             nc.scalar.activation(out=vol[:], in_=size[:], func=ACT.Sqrt, bias=spec_sb[:, c : c + 1])
             nc.sync.dma_start(out=out[c * P : (c + 1) * P, h * COLS : (h + 1) * COLS], in_=vol[:])
+
+        ys = [new_bank(i) for i in range(3)]
+        waiting = [(i, ring.tile([P, COLS], F32, name="size")) for i in range(3)]
+        for cols in (first, second):
+            for i, size in waiting:
+                second_product(i, ys[i], cols)
+                abs_on_scalar(ys[i], size, cols)
+        for i in range(3, HALVES * N_TILES, 3):
+            ys = [new_bank(i + k) for k in range(3)]
+            for k, y in enumerate(ys):
+                second_product(i + k, y, whole)
+            negated = [negate(y) for y in ys[:2]]
+            if i == 6:
+                interleave(1, whole)
+            sizes = [larger(y, minus_y) for y, minus_y in zip(ys, negated)]
+            if i == 6:
+                quantize_h(1, whole)
+            finish(*waiting.pop(0))
+            sizes.append(ring.tile([P, COLS], F32, name="size"))
+            abs_on_scalar(ys[2], sizes[2], whole)
+            for tile_and_size in waiting:
+                finish(*tile_and_size)
+            waiting = [(i + k, sizes[k]) for k in range(3)]
+        for tile_and_size in waiting:
+            finish(*tile_and_size)

@@ -1,7 +1,6 @@
 from contextlib import ExitStack
 
 import concourse.mybir as mybir
-from concourse.masks import make_identity
 
 K, T, S, H, N = 1536, 2048, 1024, 512, 1536
 FLOPS = 2 * K * H * S + 2 * H * N * S
@@ -20,13 +19,15 @@ ALU = mybir.AluOpType
 P = 128
 PACK = 4
 PASSES = K // (P * PACK)
+BANKS = 8
+DATES = S // BANKS
 COLS = 512
 HALVES = S // COLS
 N_TILES = N // P
-CHUNK = 256
-MOVED_ROWS = 100
-FIRST_ROW = 32 - 4 * PASSES
+SCALE_ROWS = 16 * PASSES
+FIRST_ROW = P - SCALE_ROWS
 STAGE_BYTES = 4 * T
+VECTOR_SHARE = (96, 32, 80)
 
 
 def tile_list_shock_factor_vols_kernel(tc, tab_words, tab_scales, offs, w1, gain, w4_words, w4_scales, spec, out):
@@ -40,139 +41,116 @@ def tile_list_shock_factor_vols_kernel(tc, tab_words, tab_scales, offs, w1, gain
         offsets = keep.tile([P, S // 16], U16, name="offsets")
         nc.sync.dma_start(offsets[:], offs)
 
-        warm = keep.tile([P, 1], F32, name="warm")
-        nc.gpsimd.memset(warm[:], 1.0)
-        identity = keep.tile([P, P], F32, name="identity")
-        make_identity(nc, identity[:])
-        spec_rows = keep.tile([P, P], F32, name="spec_rows")
-        nc.gpsimd.memset(spec_rows[:], 0.0)
-        nc.gpsimd.dma_start(out=spec_rows[0:N_TILES, :], in_=spec.rearrange("(c p) -> c p", p=P))
-        tab_plane = shared.tile([P, T], U8, name="tab_plane", align_bytes=64, offset=STAGE_BYTES - (T - N) // 2)
-        for q in range(4):
-            nc.vector.memset(tab_plane[32 * q : 32 * q + FIRST_ROW, :].bitcast(I32), 0)
+        gain_sb = keep.tile([P, PACK], F32, name="gain_sb")
+        nc.scalar.dma_start(out=gain_sb[:], in_=gain.rearrange("(p t) -> p t", t=PACK))
+
+        tab_plane = shared.tile([P, T], U8, name="tab_plane", align_bytes=64, offset=2 * STAGE_BYTES - T // 2)
+        for a in range(PASSES):
+            nc.sync.dma_start(out=tab_plane[FIRST_ROW + a : P : PASSES, :].bitcast(I32), in_=tab_scales[a].bitcast(I32))
+        nc.vector.memset(tab_plane[0:64, :].bitcast(I32), 0)
+        nc.vector.memset(tab_plane[64:FIRST_ROW, :].bitcast(I32), 0)
+        w4_plane = keep.tile([P, N], U8, name="w4_plane", align_bytes=64)
+        nc.vector.memset(w4_plane[:].bitcast(I32), 0)
+        v_planes = keep.tile([P, PASSES * S], U8, name="v_planes", align_bytes=64)
+        nc.vector.memset(v_planes[:].bitcast(I32), 0)
 
         def load_tab(a, tab):
             nc.sync.dma_start(out=tab[:], in_=tab_words[a].rearrange("p t i -> p (t i)").bitcast(I32))
             return tab
 
-        def load_w1(a, raw, queue):
+        def load_w1(a, raw):
             rows = w1[a * P * PACK : (a + 1) * P * PACK, :]
-            queue.dma_start(out=raw[:], in_=rows.rearrange("(p j) c -> p j c", j=PACK))
+            nc.sync.dma_start(out=raw[:], in_=rows.rearrange("(p j) c -> p j c", j=PACK))
             return raw
 
-        raws = [load_w1(0, keep.tile([P, PACK, H], F32, name="w1_raw0"), nc.scalar)]
-        for q, queue in enumerate((nc.sync, nc.sync, nc.sync, nc.scalar)):
-            queue.dma_start(
-                out=tab_plane[32 * q + FIRST_ROW : 32 * q + 32, :].bitcast(I32),
-                in_=tab_scales[:, 4 * q : 4 * q + 4, :].bitcast(I32),
-            )
-        warm_out = keep.tile([P, 1], F32, name="warm_out")
-        nc.scalar.activation(out=warm_out[:], in_=warm[:], func=ACT.Sqrt)
-        tabs = [load_tab(0, keep.tile([P, T], I32, name="tab0", align_bytes=64))]
-        raws.append(load_w1(1, keep.tile([P, PACK, H], F32, name="w1_raw1", tag="w1_raw1", align_bytes=64), nc.sync))
-        tabs.append(load_tab(1, keep.tile([P, T], I32, name="tab1", align_bytes=64)))
+        tabs = [load_tab(0, shared.tile([P, T], I32, name="tab0", align_bytes=64, offset=0))]
+        raws = [load_w1(0, shared.tile([P, PACK, H], F32, name="w1_raw0", align_bytes=64, offset=3 * STAGE_BYTES))]
+        raws.append(load_w1(1, keep.tile([P, PACK, H], F32, name="w1_raw1")))
 
-        v_planes = [keep.tile([P, S], U8, name=f"v_plane{a}", align_bytes=64) for a in range(PASSES)]
-        for a in range(PASSES):
-            nc.vector.memset(v_planes[a][:].bitcast(I32), 0)
-
-        gain_sb = keep.tile([P, PACK], F32, name="gain_sb")
-        nc.scalar.dma_start(out=gain_sb[:], in_=gain.rearrange("(p t) -> p t", t=PACK))
-        spec_bank = psum.tile([P, P], F32, name="spec_bank", tag="bank7")
-        nc.tensor.transpose(spec_bank[:], spec_rows[:], identity[:])
-        spec_sb = keep.tile([P, N_TILES], F32, name="spec_sb")
-        nc.scalar.copy(out=spec_sb[:], in_=spec_bank[:, 0:N_TILES])
-
-        grouped = [keep.tile([P, H * PACK], BF16, name=f"w1_grouped{a}", align_bytes=64) for a in range(PASSES)]
-        w1_codes = [keep.tile([P, H], U32, name=f"w1_codes{a}", align_bytes=64) for a in range(PASSES)]
-        f_banks = [[psum.tile([P, COLS], F32, name=f"f{h}_{t}", tag=f"bank{PACK * h + t}") for t in range(PACK)] for h in range(HALVES)]
-
-        def gather_words(a, codes, j0, j1):
-            nc.vector.tensor_copy(out=codes[:, j0:j1], in_=tabs[a][:].bitcast(U32).indirect(offsets[:, j0 // 16 : j1 // 16]))
-
-        def cast_w1(a, u, copy):
-            copy(
-                out=grouped[a][:].rearrange("p (u e m j) -> p u m e j", u=2, e=2, j=PACK)[:, u],
-                in_=raws[a][:].rearrange("p j (m u e) -> p u m e j", u=2, e=2)[:, u],
-            )
-
-        def quantize_w1(a, plane):
-            nc.vector.quantize_mx(out=w1_codes[a][:].bitcast(E4M3), scales=plane[:], in_=grouped[a][:])
-
-        def first_product(a, h):
-            for t in range(PACK):
-                nc.tensor.matmul_mx(
-                    out=f_banks[h][t][:],
-                    lhsT=w1_codes[a][:, t * P : (t + 1) * P].bitcast(E4M3),
-                    lhsT_scale=w1_planes[a][:, t * P : (t + 1) * P],
-                    rhs=v_codes[a][:, h * COLS : (h + 1) * COLS].bitcast(E5M2),
-                    rhs_scale=v_planes[a][:, h * COLS : (h + 1) * COLS],
-                    start=(a == 0),
-                    stop=(a == PASSES - 1),
-                )
-
-        picked = keep.tile([P, S], U8, name="picked", align_bytes=64)
-        nc.vector.tensor_copy(out=picked[:], in_=tab_plane[:].indirect(offsets[:]))
-
-        def move_plane(a):
-            nc.sync.dma_start(
-                out=v_planes[a][0:MOVED_ROWS, :].bitcast(I32),
-                in_=picked[FIRST_ROW + 4 * a : FIRST_ROW + 4 * a + MOVED_ROWS, :].bitcast(I32),
-            )
-
-        move_plane(0)
-        raws.append(load_w1(2, shared.tile([P, PACK, H], F32, name="w1_raw2", align_bytes=64, offset=0), nc.sync))
-        move_plane(1)
-        move_plane(2)
-        tabs.append(load_tab(2, shared.tile([P, T], I32, name="tab2", align_bytes=64, offset=STAGE_BYTES + N)))
-        w4_plane = shared.tile([P, N], U8, name="w4_plane", align_bytes=64, offset=STAGE_BYTES)
-        nc.gpsimd.memset(w4_plane[:].bitcast(I32), 0)
         for q in range(4):
-            nc.sync.dma_start(
+            nc.gpsimd.dma_start(
                 out=w4_plane[32 * q : 32 * q + 4, :].bitcast(I32),
                 in_=w4_scales[0, 4 * q : 4 * q + 4, :].bitcast(I32),
             )
 
-        v_codes = [keep.tile([P, S], U32, name=f"v_codes{a}", align_bytes=64) for a in range(PASSES)]
+        gains = keep.tile([P, DATES, PACK], F32, name="gains")
+        nc.scalar.copy(out=gains[:], in_=gain_sb[:].unsqueeze(1).to_broadcast([P, DATES, PACK]))
+
+        picked = keep.tile([P, S], U8, name="picked", align_bytes=64)
+        nc.vector.tensor_copy(out=picked[:], in_=tab_plane[:].indirect(offsets[:]))
+        rows = 4 * PASSES
+        for q, queue in enumerate((nc.sync, nc.scalar, nc.sync, nc.scalar)):
+            queue.dma_start(
+                out=v_planes[32 * q : 32 * q + 4, :].bitcast(I32),
+                in_=picked[FIRST_ROW + rows * q : FIRST_ROW + rows * (q + 1), :].bitcast(I32),
+            )
+        tabs.append(load_tab(1, shared.tile([P, T], I32, name="tab1", align_bytes=64, offset=STAGE_BYTES)))
+        raws.append(load_w1(2, shared.tile([P, PACK, H], F32, name="w1_raw2", align_bytes=64, offset=2 * STAGE_BYTES)))
+
+        grouped = [keep.tile([P, H * PACK], BF16, name=f"w1_grouped{a}", align_bytes=64) for a in range(PASSES)]
+        w1_codes = [keep.tile([P, H], U32, name=f"w1_codes{a}", align_bytes=64) for a in range(PASSES)]
         w1_planes = [keep.tile([P, H], U8, name=f"w1_plane{a}", align_bytes=64) for a in range(PASSES)]
-        for a in range(PASSES - 1):
-            cast_w1(a, 0, nc.scalar.copy)
-            cast_w1(a, 1, nc.scalar.copy)
-            gather_words(a, v_codes[a], 0, S)
-            quantize_w1(a, w1_planes[a])
-            first_product(a, 0)
-            first_product(a, 1)
-        w4_codes = keep.tile([P, N], I32, name="w4_codes", tag="w1_raw1", align_bytes=64)
-        nc.sync.dma_start(out=w4_codes[:], in_=w4_words[0].rearrange("p c i -> p (c i)").bitcast(I32))
-        cast_w1(2, 0, nc.vector.tensor_copy)
-        cast_w1(2, 1, nc.scalar.copy)
-        quantize_w1(2, w1_planes[2])
-        for h in range(HALVES):
-            gather_words(2, v_codes[2], h * COLS, (h + 1) * COLS)
-            first_product(2, h)
+        v_codes = [keep.tile([P, S], U32, name=f"v_codes{a}", align_bytes=64) for a in range(PASSES)]
+        f_banks = [psum.tile([P, PACK, DATES], F32, name=f"f{b}", tag=f"bank{b}") for b in range(BANKS)]
 
-        squares = [keep.tile([P, PACK, COLS], F32, name=f"squares{h}", align_bytes=64) for h in range(HALVES)]
-        h_grouped = [keep.tile([P, COLS * PACK], BF16, name=f"h_grouped{h}", tag=f"h_grouped{h}", align_bytes=64) for h in range(HALVES)]
-        h_codes = [keep.tile([P, COLS], U32, name=f"h_codes{h}", align_bytes=64) for h in range(HALVES)]
-        h_planes = [keep.tile([P, COLS], U8, name=f"h_plane{h}", align_bytes=64) for h in range(HALVES)]
-        h_rows = [keep.tile([P, PACK, COLS], BF16, name="h_rows0", align_bytes=64)]
+        def gather_words(a, j0, j1):
+            nc.vector.tensor_copy(out=v_codes[a][:, j0:j1], in_=tabs[a][:].bitcast(U32).indirect(offsets[:, j0 // 16 : j1 // 16]))
 
-        for h, width in enumerate((CHUNK, COLS)):
-            for c0 in range(0, COLS, width):
-                for t in range(PACK):
-                    nc.scalar.activation(out=squares[h][:, t, c0 : c0 + width], in_=f_banks[h][t][:, c0 : c0 + width], func=ACT.Square)
+        def quantize_w1(a):
+            dst = grouped[a][:].rearrange("p (t m j) -> p m t j", t=PACK, j=PACK)
+            src = raws[a][:].rearrange("p j (m t) -> p m t j", t=PACK)
+            cut = VECTOR_SHARE[a]
+            nc.scalar.copy(out=dst[:, cut:P], in_=src[:, cut:P])
+            nc.vector.tensor_copy(out=dst[:, 0:cut], in_=src[:, 0:cut])
+            nc.vector.quantize_mx(out=w1_codes[a][:].bitcast(E4M3), scales=w1_planes[a][:], in_=grouped[a][:])
 
-        def weigh(h, cols, engine):
+        def first_product(a, b):
             for t in range(PACK):
-                engine.tensor_scalar(
-                    out=h_rows[h][:, t, cols], in0=squares[h][:, t, cols],
-                    scalar1=gain_sb[:, t : t + 1], scalar2=0.0, op0=ALU.mult, op1=ALU.add,
+                nc.tensor.matmul_mx(
+                    out=f_banks[b][:, t, :],
+                    lhsT=w1_codes[a][:, t * P : (t + 1) * P].bitcast(E4M3),
+                    lhsT_scale=w1_planes[a][:, t * P : (t + 1) * P],
+                    rhs=v_codes[a][:, b * DATES : (b + 1) * DATES].bitcast(E5M2),
+                    rhs_scale=v_planes[:, a * S + b * DATES : a * S + (b + 1) * DATES],
+                    start=(a == 0 and t == 0),
+                    stop=(a == PASSES - 1 and t == PACK - 1),
                 )
 
-        def interleave(h, cols):
-            nc.vector.tensor_copy(
-                out=h_grouped[h][:].rearrange("p (c t) -> p c t", t=PACK)[:, cols],
-                in_=h_rows[h][:].rearrange("p t c -> p c t")[:, cols],
+        gather_words(0, 0, S)
+        tabs.append(load_tab(2, shared.tile([P, T], I32, name="tab2", align_bytes=64, offset=0)))
+        quantize_w1(0)
+        w4_codes = shared.tile([P, N], I32, name="w4_codes", align_bytes=64, offset=3 * STAGE_BYTES)
+        nc.sync.dma_start(out=w4_codes[:], in_=w4_words[0].rearrange("p c i -> p (c i)").bitcast(I32))
+        spec_sb = shared.tile([P, N_TILES], F32, name="spec_sb", align_bytes=64, offset=3 * STAGE_BYTES + 4 * N)
+        with nc.allow_non_contiguous_dma(reason="one value of spec for each partition and output tile"):
+            nc.sync.dma_start(out=spec_sb[:], in_=spec.rearrange("(c p) -> p c", p=P))
+        for b in range(BANKS):
+            first_product(0, b)
+        quantize_w1(1)
+        for h in range(HALVES):
+            gather_words(1, h * COLS, (h + 1) * COLS)
+            for b in range(h * PACK, (h + 1) * PACK):
+                first_product(1, b)
+        quantize_w1(2)
+
+        squares = [keep.tile([P, DATES, PACK], F32, name=f"squares{b}", align_bytes=64) for b in range(BANKS)]
+        h_grouped = [keep.tile([P, COLS * PACK], BF16, name="h_grouped0", tag="h_grouped", align_bytes=64)]
+        h_codes = [keep.tile([P, COLS], U32, name=f"h_codes{h}", align_bytes=64) for h in range(HALVES)]
+        h_planes = [keep.tile([P, COLS], U8, name=f"h_plane{h}", align_bytes=64) for h in range(HALVES)]
+
+        for b in range(BANKS):
+            if b % 2 == 0:
+                gather_words(2, b * DATES, (b + 2) * DATES)
+            first_product(2, b)
+            nc.scalar.activation(out=squares[b][:], in_=f_banks[b][:].rearrange("p t j -> p j t"), func=ACT.Square)
+
+        def weigh(b, engine):
+            h, i = divmod(b, PACK)
+            engine.tensor_tensor(
+                out=h_grouped[h][:, i * COLS : (i + 1) * COLS],
+                in0=squares[b][:].rearrange("p j t -> p (j t)"),
+                in1=gains[:].rearrange("p j t -> p (j t)"),
+                op=ALU.mult,
             )
 
         def quantize_h(h, cols):
@@ -182,33 +160,33 @@ def tile_list_shock_factor_vols_kernel(tc, tab_words, tab_scales, offs, w1, gain
                 in_=h_grouped[h][:, cols.start * PACK : cols.stop * PACK],
             )
 
-        first, second, whole = slice(0, CHUNK), slice(CHUNK, COLS), slice(0, COLS)
-        weigh(0, first, nc.vector)
-        interleave(0, first)
-        weigh(0, second, nc.vector)
-        quantize_h(0, first)
-        interleave(0, second)
-        quantize_h(0, second)
-        h_rows.append(keep.tile([P, PACK, COLS], BF16, name="h_rows1", tag="h_grouped0", align_bytes=64))
-        weigh(1, whole, nc.gpsimd)
+        for b in range(3):
+            weigh(b, nc.vector)
+        quantize_h(0, slice(0, 2 * DATES))
+        weigh(3, nc.vector)
+        quantize_h(0, slice(2 * DATES, COLS))
+        h_grouped.append(keep.tile([P, COLS * PACK], BF16, name="h_grouped1", tag="h_grouped", align_bytes=64))
+        for b in range(PACK, BANKS):
+            weigh(b, nc.gpsimd)
 
-        def second_product(i, y, cols):
+        def second_product(i):
             h, c = divmod(i, N_TILES)
+            y = psum.tile([P, COLS], F32, name=f"y{i}", tag=f"bank{i % BANKS}")
             nc.tensor.matmul_mx(
-                out=y[:, cols],
+                out=y[:],
                 lhsT=w4_codes[:, c * P : (c + 1) * P].bitcast(E4M3),
                 lhsT_scale=w4_plane[:, c * P : (c + 1) * P],
-                rhs=h_codes[h][:, cols].bitcast(E4M3),
-                rhs_scale=h_planes[h][:, cols],
+                rhs=h_codes[h][:].bitcast(E4M3),
+                rhs_scale=h_planes[h][:],
                 start=True,
                 stop=True,
             )
+            return y
 
-        def new_bank(i):
-            return psum.tile([P, COLS], F32, name=f"y{i}", tag=f"bank{i % 8}")
-
-        def abs_on_scalar(y, size, cols):
-            nc.scalar.activation(out=size[:, cols], in_=y[:, cols], func=ACT.Abs)
+        def abs_on_scalar(y):
+            size = ring.tile([P, COLS], F32, name="size")
+            nc.scalar.activation(out=size[:], in_=y[:], func=ACT.Abs)
+            return size
 
         def negate(y):
             minus_y = ring.tile([P, COLS], F32, name="minus_y")
@@ -226,25 +204,14 @@ def tile_list_shock_factor_vols_kernel(tc, tab_words, tab_scales, offs, w1, gain
             nc.scalar.activation(out=vol[:], in_=size[:], func=ACT.Sqrt, bias=spec_sb[:, c : c + 1])
             nc.sync.dma_start(out=out[c * P : (c + 1) * P, h * COLS : (h + 1) * COLS], in_=vol[:])
 
-        ys = [new_bank(i) for i in range(3)]
-        waiting = [(i, ring.tile([P, COLS], F32, name="size")) for i in range(3)]
-        for cols in (first, second):
-            for i, size in waiting:
-                second_product(i, ys[i], cols)
-                abs_on_scalar(ys[i], size, cols)
-        for i in range(3, HALVES * N_TILES, 3):
-            ys = [new_bank(i + k) for k in range(3)]
-            for k, y in enumerate(ys):
-                second_product(i + k, y, whole)
+        waiting = []
+        for i in range(0, HALVES * N_TILES, 3):
+            ys = [second_product(i + k) for k in range(3)]
             negated = [negate(y) for y in ys[:2]]
             if i == 6:
-                interleave(1, whole)
+                quantize_h(1, slice(0, COLS))
             sizes = [larger(y, minus_y) for y, minus_y in zip(ys, negated)]
-            if i == 6:
-                quantize_h(1, whole)
-            finish(*waiting.pop(0))
-            sizes.append(ring.tile([P, COLS], F32, name="size"))
-            abs_on_scalar(ys[2], sizes[2], whole)
+            sizes.append(abs_on_scalar(ys[2]))
             for tile_and_size in waiting:
                 finish(*tile_and_size)
             waiting = [(i + k, sizes[k]) for k in range(3)]

@@ -1,6 +1,7 @@
 from contextlib import ExitStack
 
 import concourse.mybir as mybir
+from concourse.masks import make_identity
 
 K, T, S, H, N = 1536, 2048, 1024, 512, 1536
 FLOPS = 2 * K * H * S + 2 * H * N * S
@@ -27,6 +28,7 @@ N_TILES = N // P
 SCALE_ROWS = 16 * PASSES
 FIRST_ROW = P - SCALE_ROWS
 STAGE_BYTES = 4 * T
+EARLY = 9
 VECTOR_SHARE = (96, 32, 80)
 
 
@@ -42,7 +44,12 @@ def tile_list_shock_factor_vols_kernel(tc, tab_words, tab_scales, offs, w1, gain
         nc.sync.dma_start(offsets[:], offs)
 
         gain_sb = keep.tile([P, PACK], F32, name="gain_sb")
-        nc.scalar.dma_start(out=gain_sb[:], in_=gain.rearrange("(p t) -> p t", t=PACK))
+
+        spec_rows = keep.tile([P, P], F32, name="spec_rows")
+        nc.gpsimd.memset(spec_rows[0:96, :], 0.0)
+        nc.gpsimd.memset(spec_rows[96 : P - N_TILES, :], 0.0)
+        identity = keep.tile([P, P], F32, name="identity")
+        make_identity(nc, identity[:])
 
         tab_plane = shared.tile([P, T], U8, name="tab_plane", align_bytes=64, offset=2 * STAGE_BYTES - T // 2)
         for a in range(PASSES):
@@ -64,6 +71,8 @@ def tile_list_shock_factor_vols_kernel(tc, tab_words, tab_scales, offs, w1, gain
             return raw
 
         tabs = [load_tab(0, shared.tile([P, T], I32, name="tab0", align_bytes=64, offset=0))]
+        nc.sync.dma_start(out=gain_sb[:], in_=gain.rearrange("(p t) -> p t", t=PACK))
+        nc.sync.dma_start(out=spec_rows[P - N_TILES : P, :], in_=spec.rearrange("(c p) -> c p", p=P))
         raws = [load_w1(0, shared.tile([P, PACK, H], F32, name="w1_raw0", align_bytes=64, offset=3 * STAGE_BYTES))]
         raws.append(load_w1(1, keep.tile([P, PACK, H], F32, name="w1_raw1")))
 
@@ -75,6 +84,11 @@ def tile_list_shock_factor_vols_kernel(tc, tab_words, tab_scales, offs, w1, gain
 
         gains = keep.tile([P, DATES, PACK], F32, name="gains")
         nc.scalar.copy(out=gains[:], in_=gain_sb[:].unsqueeze(1).to_broadcast([P, DATES, PACK]))
+
+        spec_bank = psum.tile([P, P], F32, name="spec_bank", tag="bank7")
+        nc.tensor.transpose(spec_bank[:], spec_rows[:], identity[:])
+        spec_sb = keep.tile([P, N_TILES], F32, name="spec_sb")
+        nc.scalar.copy(out=spec_sb[:], in_=spec_bank[:, P - N_TILES : P])
 
         picked = keep.tile([P, S], U8, name="picked", align_bytes=64)
         nc.vector.tensor_copy(out=picked[:], in_=tab_plane[:].indirect(offsets[:]))
@@ -97,8 +111,8 @@ def tile_list_shock_factor_vols_kernel(tc, tab_words, tab_scales, offs, w1, gain
             nc.vector.tensor_copy(out=v_codes[a][:, j0:j1], in_=tabs[a][:].bitcast(U32).indirect(offsets[:, j0 // 16 : j1 // 16]))
 
         def quantize_w1(a):
-            dst = grouped[a][:].rearrange("p (t m j) -> p m t j", t=PACK, j=PACK)
-            src = raws[a][:].rearrange("p j (m t) -> p m t j", t=PACK)
+            dst = grouped[a][:].rearrange("p (t m j) -> p m j t", t=PACK, j=PACK)
+            src = raws[a][:].rearrange("p j (m t) -> p m j t", t=PACK)
             cut = VECTOR_SHARE[a]
             nc.scalar.copy(out=dst[:, cut:P], in_=src[:, cut:P])
             nc.vector.tensor_copy(out=dst[:, 0:cut], in_=src[:, 0:cut])
@@ -121,9 +135,6 @@ def tile_list_shock_factor_vols_kernel(tc, tab_words, tab_scales, offs, w1, gain
         quantize_w1(0)
         w4_codes = shared.tile([P, N], I32, name="w4_codes", align_bytes=64, offset=3 * STAGE_BYTES)
         nc.sync.dma_start(out=w4_codes[:], in_=w4_words[0].rearrange("p c i -> p (c i)").bitcast(I32))
-        spec_sb = shared.tile([P, N_TILES], F32, name="spec_sb", align_bytes=64, offset=3 * STAGE_BYTES + 4 * N)
-        with nc.allow_non_contiguous_dma(reason="one value of spec for each partition and output tile"):
-            nc.sync.dma_start(out=spec_sb[:], in_=spec.rearrange("(c p) -> p c", p=P))
         for b in range(BANKS):
             first_product(0, b)
         quantize_w1(1)
@@ -169,8 +180,11 @@ def tile_list_shock_factor_vols_kernel(tc, tab_words, tab_scales, offs, w1, gain
         for b in range(PACK, BANKS):
             weigh(b, nc.gpsimd)
 
+        order = [(h, c) for h in range(HALVES) for c in range(EARLY)] + [(h, c) for c in range(EARLY, N_TILES) for h in range(HALVES)]
+        vols = [keep.tile([P, S], F32, name=f"vol{c}") for c in range(N_TILES)]
+
         def second_product(i):
-            h, c = divmod(i, N_TILES)
+            h, c = order[i]
             y = psum.tile([P, COLS], F32, name=f"y{i}", tag=f"bank{i % BANKS}")
             nc.tensor.matmul_mx(
                 out=y[:],
@@ -199,10 +213,13 @@ def tile_list_shock_factor_vols_kernel(tc, tab_words, tab_scales, offs, w1, gain
             return size
 
         def finish(i, size):
-            h, c = divmod(i, N_TILES)
-            vol = keep.tile([P, COLS], F32, name=f"vol{i}")
-            nc.scalar.activation(out=vol[:], in_=size[:], func=ACT.Sqrt, bias=spec_sb[:, c : c + 1])
-            nc.sync.dma_start(out=out[c * P : (c + 1) * P, h * COLS : (h + 1) * COLS], in_=vol[:])
+            h, c = order[i]
+            cols = slice(h * COLS, (h + 1) * COLS)
+            nc.scalar.activation(out=vols[c][:, cols], in_=size[:], func=ACT.Sqrt, bias=spec_sb[:, c : c + 1])
+            if c < EARLY or c == N_TILES - 1:
+                nc.sync.dma_start(out=out[c * P : (c + 1) * P, cols], in_=vols[c][:, cols])
+            elif h == HALVES - 1:
+                nc.sync.dma_start(out=out[c * P : (c + 1) * P, :], in_=vols[c][:])
 
         waiting = []
         for i in range(0, HALVES * N_TILES, 3):

@@ -43,6 +43,11 @@ def tile_list_shock_factor_vols_kernel(tc, tab_words, tab_scales, offs, w1, gain
         offsets = keep.tile([P, S // 16], U16, name="offsets")
         nc.sync.dma_start(offsets[:], offs)
 
+        warm = keep.tile([P, 1], F32, name="warm")
+        nc.gpsimd.memset(warm[:], 1.0)
+        warm_out = keep.tile([P, 1], F32, name="warm_out")
+        nc.scalar.activation(out=warm_out[:], in_=warm[:], func=ACT.Sqrt)
+
         gain_sb = keep.tile([P, PACK], F32, name="gain_sb")
 
         spec_rows = keep.tile([P, P], F32, name="spec_rows")

@@ -27,9 +27,9 @@ HALVES = S // COLS
 N_TILES = N // P
 SCALE_ROWS = 16 * PASSES
 FIRST_ROW = P - SCALE_ROWS
+LAST_ROWS = P - 16
 STAGE_BYTES = 4 * T
-EARLY = 9
-VECTOR_SHARE = (96, 32, 80)
+VECTOR_SHARE = (48, 48, 72)
 
 
 def tile_list_shock_factor_vols_kernel(tc, tab_words, tab_scales, offs, w1, gain, w4_words, w4_scales, spec, out):
@@ -57,8 +57,8 @@ def tile_list_shock_factor_vols_kernel(tc, tab_words, tab_scales, offs, w1, gain
         make_identity(nc, identity[:])
 
         tab_plane = shared.tile([P, T], U8, name="tab_plane", align_bytes=64, offset=2 * STAGE_BYTES - T // 2)
-        for a in range(PASSES):
-            nc.sync.dma_start(out=tab_plane[FIRST_ROW + a : P : PASSES, :].bitcast(I32), in_=tab_scales[a].bitcast(I32))
+        for a, rows in enumerate((slice(FIRST_ROW, LAST_ROWS, 2), slice(FIRST_ROW + 1, LAST_ROWS, 2), slice(LAST_ROWS, P))):
+            nc.sync.dma_start(out=tab_plane[rows, :].bitcast(I32), in_=tab_scales[a].bitcast(I32))
         nc.vector.memset(tab_plane[0:64, :].bitcast(I32), 0)
         nc.vector.memset(tab_plane[64:FIRST_ROW, :].bitcast(I32), 0)
         w4_plane = keep.tile([P, N], U8, name="w4_plane", align_bytes=64)
@@ -75,11 +75,11 @@ def tile_list_shock_factor_vols_kernel(tc, tab_words, tab_scales, offs, w1, gain
             nc.sync.dma_start(out=raw[:], in_=rows.rearrange("(p j) c -> p j c", j=PACK))
             return raw
 
-        tabs = [load_tab(0, shared.tile([P, T], I32, name="tab0", align_bytes=64, offset=0))]
+        raws = [load_w1(0, keep.tile([P, PACK, H], F32, name="w1_raw0"))]
         nc.sync.dma_start(out=gain_sb[:], in_=gain.rearrange("(p t) -> p t", t=PACK))
         nc.sync.dma_start(out=spec_rows[P - N_TILES : P, :], in_=spec.rearrange("(c p) -> c p", p=P))
-        raws = [load_w1(0, shared.tile([P, PACK, H], F32, name="w1_raw0", align_bytes=64, offset=3 * STAGE_BYTES))]
-        raws.append(load_w1(1, keep.tile([P, PACK, H], F32, name="w1_raw1")))
+        tabs = [load_tab(0, shared.tile([P, T], I32, name="tab0", align_bytes=64, offset=0))]
+        raws.append(load_w1(1, shared.tile([P, PACK, H], F32, name="w1_raw1", align_bytes=64, offset=3 * STAGE_BYTES)))
 
         for q in range(4):
             nc.gpsimd.dma_start(
@@ -97,14 +97,19 @@ def tile_list_shock_factor_vols_kernel(tc, tab_words, tab_scales, offs, w1, gain
 
         picked = keep.tile([P, S], U8, name="picked", align_bytes=64)
         nc.vector.tensor_copy(out=picked[:], in_=tab_plane[:].indirect(offsets[:]))
-        rows = 4 * PASSES
-        for q, queue in enumerate((nc.sync, nc.scalar, nc.sync, nc.scalar)):
-            queue.dma_start(
-                out=v_planes[32 * q : 32 * q + 4, :].bitcast(I32),
-                in_=picked[FIRST_ROW + rows * q : FIRST_ROW + rows * (q + 1), :].bitcast(I32),
-            )
+
+        def move_planes(first_row, passes, first_pass):
+            for q in range(4):
+                row = first_row + 4 * passes * q
+                nc.sync.dma_start(
+                    out=v_planes[32 * q : 32 * q + 4, first_pass * S : (first_pass + passes) * S].bitcast(I32),
+                    in_=picked[row : row + 4 * passes, :].bitcast(I32),
+                )
+
+        move_planes(FIRST_ROW, 2, 0)
         tabs.append(load_tab(1, shared.tile([P, T], I32, name="tab1", align_bytes=64, offset=STAGE_BYTES)))
         raws.append(load_w1(2, shared.tile([P, PACK, H], F32, name="w1_raw2", align_bytes=64, offset=2 * STAGE_BYTES)))
+        move_planes(LAST_ROWS, 1, 2)
 
         grouped = [keep.tile([P, H * PACK], BF16, name=f"w1_grouped{a}", align_bytes=64) for a in range(PASSES)]
         w1_codes = [keep.tile([P, H], U32, name=f"w1_codes{a}", align_bytes=64) for a in range(PASSES)]
@@ -138,11 +143,11 @@ def tile_list_shock_factor_vols_kernel(tc, tab_words, tab_scales, offs, w1, gain
         gather_words(0, 0, S)
         tabs.append(load_tab(2, shared.tile([P, T], I32, name="tab2", align_bytes=64, offset=0)))
         quantize_w1(0)
-        w4_codes = shared.tile([P, N], I32, name="w4_codes", align_bytes=64, offset=3 * STAGE_BYTES)
-        nc.sync.dma_start(out=w4_codes[:], in_=w4_words[0].rearrange("p c i -> p (c i)").bitcast(I32))
         for b in range(BANKS):
             first_product(0, b)
         quantize_w1(1)
+        w4_codes = shared.tile([P, N], I32, name="w4_codes", align_bytes=64, offset=3 * STAGE_BYTES)
+        nc.sync.dma_start(out=w4_codes[:], in_=w4_words[0].rearrange("p c i -> p (c i)").bitcast(I32))
         for h in range(HALVES):
             gather_words(1, h * COLS, (h + 1) * COLS)
             for b in range(h * PACK, (h + 1) * PACK):
@@ -185,57 +190,85 @@ def tile_list_shock_factor_vols_kernel(tc, tab_words, tab_scales, offs, w1, gain
         for b in range(PACK, BANKS):
             weigh(b, nc.gpsimd)
 
-        order = [(h, c) for h in range(HALVES) for c in range(EARLY)] + [(h, c) for c in range(EARLY, N_TILES) for h in range(HALVES)]
-        vols = [keep.tile([P, S], F32, name=f"vol{c}") for c in range(N_TILES)]
+        for_scalar, for_vector = [], []
 
-        def second_product(i):
-            h, c = order[i]
-            y = psum.tile([P, COLS], F32, name=f"y{i}", tag=f"bank{i % BANKS}")
+        def new_bank(made, first_bank):
+            made.append(psum.tile([P, COLS], F32, name=f"y{first_bank}_{len(made)}", tag=f"bank{first_bank + len(made) % (BANKS // 2)}"))
+            return made[-1]
+
+        def second_product(y, i, cols):
+            h, c = divmod(i, N_TILES)
             nc.tensor.matmul_mx(
-                out=y[:],
+                out=y,
                 lhsT=w4_codes[:, c * P : (c + 1) * P].bitcast(E4M3),
                 lhsT_scale=w4_plane[:, c * P : (c + 1) * P],
-                rhs=h_codes[h][:].bitcast(E4M3),
-                rhs_scale=h_planes[h][:],
+                rhs=h_codes[h][:, cols].bitcast(E4M3),
+                rhs_scale=h_planes[h][:, cols],
                 start=True,
                 stop=True,
             )
-            return y
 
-        def abs_on_scalar(y):
-            size = ring.tile([P, COLS], F32, name="size")
-            nc.scalar.activation(out=size[:], in_=y[:], func=ACT.Abs)
-            return size
+        vols = keep.tile([P, HALVES * N_TILES, COLS], F32, name="vols")
+        whole = slice(0, COLS)
+        chunks = (slice(0, COLS // 2), slice(COLS // 2, COLS))
 
-        def negate(y):
-            minus_y = ring.tile([P, COLS], F32, name="minus_y")
-            nc.vector.tensor_scalar_mul(out=minus_y[:], in0=y[:], scalar1=-1.0)
-            return minus_y
+        def products(made, first_bank, i, cols):
+            y = new_bank(made, first_bank)
+            tiles = COLS // (cols.stop - cols.start)
+            view = y[:].rearrange("p (k j) -> p k j", k=tiles)
+            for k in range(tiles):
+                second_product(view[:, k], i + k, cols)
+            return view, vols[:, i : i + tiles, cols]
 
-        def larger(y, minus_y):
-            size = ring.tile([P, COLS], F32, name="size")
-            nc.vector.tensor_tensor(out=size[:], in0=y[:], in1=minus_y[:], op=ALU.max)
-            return size
+        def abs_on_scalar(i, cols):
+            y, size = products(for_scalar, 0, i, cols)
+            nc.scalar.activation(out=size, in_=y, func=ACT.Abs)
 
-        def finish(i, size):
-            h, c = order[i]
-            cols = slice(h * COLS, (h + 1) * COLS)
-            nc.scalar.activation(out=vols[c][:, cols], in_=size[:], func=ACT.Sqrt, bias=spec_sb[:, c : c + 1])
-            if c < EARLY or c == N_TILES - 1:
-                nc.sync.dma_start(out=out[c * P : (c + 1) * P, cols], in_=vols[c][:, cols])
-            elif h == HALVES - 1:
-                nc.sync.dma_start(out=out[c * P : (c + 1) * P, :], in_=vols[c][:])
+        def negate(i, cols):
+            y, size = products(for_vector, BANKS // 2, i, cols)
+            minus_y = ring.tile(list(y.shape), F32, name="minus_y")
+            nc.vector.tensor_scalar_mul(out=minus_y[:], in0=y, scalar1=-1.0)
+            return y, minus_y[:], size
 
-        waiting = []
-        for i in range(0, HALVES * N_TILES, 3):
-            ys = [second_product(i + k) for k in range(3)]
-            negated = [negate(y) for y in ys[:2]]
-            if i == 6:
-                quantize_h(1, slice(0, COLS))
-            sizes = [larger(y, minus_y) for y, minus_y in zip(ys, negated)]
-            sizes.append(abs_on_scalar(ys[2]))
-            for tile_and_size in waiting:
-                finish(*tile_and_size)
-            waiting = [(i + k, sizes[k]) for k in range(3)]
-        for tile_and_size in waiting:
-            finish(*tile_and_size)
+        def larger(y, minus_y, size, cols):
+            nc.vector.tensor_tensor(out=size[:, :, cols], in0=y[:, :, cols], in1=minus_y[:, :, cols], op=ALU.max)
+
+        def finish(i, cols):
+            h, c = divmod(i, N_TILES)
+            nc.scalar.activation(out=vols[:, i, cols], in_=vols[:, i, cols], func=ACT.Sqrt, bias=spec_sb[:, c : c + 1])
+            nc.sync.dma_start(out=out[c * P : (c + 1) * P, h * COLS + cols.start : h * COLS + cols.stop], in_=vols[:, i, cols])
+
+        negated = []
+        for cols in chunks:
+            abs_on_scalar(0, cols)
+            negated.append(negate(2, cols))
+        for made in negated:
+            larger(*made, chunks[0])
+        finish(0, whole)
+        finish(1, whole)
+        groups = ((1, 2), (1, 2), (1, 1), (2, 2), (1, 2), (1, 2), (0, 2))
+        i = 4
+        waiting = [2, 3]
+        for own, other in groups:
+            scalars = range(i, i + own)
+            vectors = range(i + own, i + own + other)
+            i = i + own + other
+            negated = [negate(k, whole) for k in vectors]
+            for k in scalars:
+                abs_on_scalar(k, whole)
+            if i == N_TILES:
+                quantize_h(1, whole)
+            for k in waiting:
+                finish(k, whole)
+            for k in scalars:
+                finish(k, whole)
+            waiting = list(vectors)
+            if i == HALVES * N_TILES:
+                larger(*negated[0], whole)
+                finish(vectors[0], whole)
+                for cols in chunks:
+                    larger(*negated[1], cols)
+                    finish(vectors[1], cols)
+            else:
+                for made in negated:
+                    larger(*made, whole)

@@ -29,6 +29,7 @@ SCALE_ROWS = 16 * PASSES
 FIRST_ROW = P - SCALE_ROWS
 LAST_ROWS = P - 16
 STAGE_BYTES = 4 * T
+LARGEST = 3.4028234663852886e38
 VECTOR_SHARE = (48, 48, 72)
 
 
@@ -233,42 +234,63 @@ def tile_list_shock_factor_vols_kernel(tc, tab_words, tab_scales, offs, w1, gain
         def larger(y, minus_y, size, cols):
             nc.vector.tensor_tensor(out=size[:, :, cols], in0=y[:, :, cols], in1=minus_y[:, :, cols], op=ALU.max)
 
-        def finish(i, cols):
+        def halve(i):
+            y, size = products(for_vector, BANKS // 2, i, whole)
+            half_y = ring.tile([P, COLS], F32, name="half_y")
+            nc.vector.tensor_scalar_mul(out=half_y[:], in0=y[:, 0], scalar1=0.5)
+            return half_y, size[:, 0]
+
+        def abs_on_gpsimd(half_y, size):
+            positive = keep.tile([P, COLS], F32, name="positive", tag="h_grouped", align_bytes=64)
+            nc.gpsimd.tensor_scalar(out=positive[:], in0=half_y[:], scalar1=LARGEST, scalar2=0.0, op0=ALU.min, op1=ALU.max)
+            nc.gpsimd.tensor_scalar(out=positive[:], in0=positive[:], scalar1=2.0, scalar2=0.0, op0=ALU.mult, op1=ALU.add)
+            nc.gpsimd.tensor_tensor(out=size, in0=positive[:], in1=half_y[:], op=ALU.subtract)
+
+        def finish(i, cols, scale=1.0):
             h, c = divmod(i, N_TILES)
-            nc.scalar.activation(out=vols[:, i, cols], in_=vols[:, i, cols], func=ACT.Sqrt, bias=spec_sb[:, c : c + 1])
+            nc.scalar.activation(out=vols[:, i, cols], in_=vols[:, i, cols], func=ACT.Sqrt, bias=spec_sb[:, c : c + 1], scale=scale)
             nc.sync.dma_start(out=out[c * P : (c + 1) * P, h * COLS + cols.start : h * COLS + cols.stop], in_=vols[:, i, cols])
 
-        negated = []
-        for cols in chunks:
-            abs_on_scalar(0, cols)
-            negated.append(negate(2, cols))
-        for made in negated:
-            larger(*made, chunks[0])
+        abs_on_scalar(0, chunks[0])
+        abs_on_scalar(2, chunks[0])
+        made = negate(2, chunks[1])
+        abs_on_scalar(0, chunks[1])
+        larger(*made, chunks[0])
         finish(0, whole)
         finish(1, whole)
-        groups = ((1, 2), (1, 2), (1, 1), (2, 2), (1, 2), (1, 2), (0, 2))
+        groups = ((1, 2, 0), (0, 2, 1), (1, 0, 1), (1, 2, 0), (1, 1, 1), (1, 2, 0), (0, 2, 0))
         i = 4
         waiting = [2, 3]
-        for own, other in groups:
+        slow = [[], []]
+        for g, (own, other, third) in enumerate(groups):
             scalars = range(i, i + own)
             vectors = range(i + own, i + own + other)
-            i = i + own + other
+            gpsimds = range(i + own + other, i + own + other + third)
+            i = i + own + other + third
+            halved = [halve(k) for k in gpsimds]
             negated = [negate(k, whole) for k in vectors]
             for k in scalars:
                 abs_on_scalar(k, whole)
-            if i == N_TILES:
+            if g == 1:
                 quantize_h(1, whole)
+            for made in halved:
+                abs_on_gpsimd(*made)
             for k in waiting:
                 finish(k, whole)
             for k in scalars:
                 finish(k, whole)
+            for k in slow.pop(0):
+                finish(k, whole, 2.0)
+            slow.append(gpsimds)
             waiting = list(vectors)
-            if i == HALVES * N_TILES:
-                larger(*negated[0], whole)
-                finish(vectors[0], whole)
-                for cols in chunks:
-                    larger(*negated[1], cols)
-                    finish(vectors[1], cols)
-            else:
-                for made in negated:
-                    larger(*made, whole)
+            for made in negated:
+                larger(*made, whole)
+        y, size = products(for_vector, BANKS // 2, i, whole)
+        minus_y = ring.tile([P, 1, COLS], F32, name="minus_y")
+        for cols in chunks:
+            nc.vector.tensor_scalar_mul(out=minus_y[:, :, cols], in0=y[:, :, cols], scalar1=-1.0)
+        for k in waiting:
+            finish(k, whole)
+        for cols in chunks:
+            larger(y, minus_y[:], size, cols)
+            finish(i, cols)

@@ -49,7 +49,6 @@ def tile_list_shock_factor_vols_kernel(tc, tab_words, tab_scales, offs, w1, gain
         warm_out = keep.tile([P, 1], F32, name="warm_out")
         nc.scalar.activation(out=warm_out[:], in_=warm[:], func=ACT.Sqrt)
 
-        gain_sb = keep.tile([P, PACK], F32, name="gain_sb")
 
         spec_rows = keep.tile([P, P], F32, name="spec_rows")
         nc.gpsimd.memset(spec_rows[0:96, :], 0.0)
@@ -58,12 +57,13 @@ def tile_list_shock_factor_vols_kernel(tc, tab_words, tab_scales, offs, w1, gain
         make_identity(nc, identity[:])
 
         tab_plane = shared.tile([P, T], U8, name="tab_plane", align_bytes=64, offset=2 * STAGE_BYTES - T // 2)
-        for a, rows in enumerate((slice(FIRST_ROW, LAST_ROWS, 2), slice(FIRST_ROW + 1, LAST_ROWS, 2), slice(LAST_ROWS, P))):
-            nc.sync.dma_start(out=tab_plane[rows, :].bitcast(I32), in_=tab_scales[a].bitcast(I32))
+        nc.sync.dma_start(
+            out=tab_plane[FIRST_ROW:LAST_ROWS, :].bitcast(I32),
+            in_=tab_scales[0:2].rearrange("a q t -> q a t").bitcast(I32),
+        )
+        nc.sync.dma_start(out=tab_plane[LAST_ROWS:P, :].bitcast(I32), in_=tab_scales[2].bitcast(I32))
         nc.vector.memset(tab_plane[0:64, :].bitcast(I32), 0)
         nc.vector.memset(tab_plane[64:FIRST_ROW, :].bitcast(I32), 0)
-        w4_plane = keep.tile([P, N], U8, name="w4_plane", align_bytes=64)
-        nc.vector.memset(w4_plane[:].bitcast(I32), 0)
         v_planes = keep.tile([P, PASSES * S], U8, name="v_planes", align_bytes=64)
         nc.vector.memset(v_planes[:].bitcast(I32), 0)
 
@@ -77,19 +77,14 @@ def tile_list_shock_factor_vols_kernel(tc, tab_words, tab_scales, offs, w1, gain
             return raw
 
         raws = [load_w1(0, keep.tile([P, PACK, H], F32, name="w1_raw0"))]
+        gain_sb = keep.tile([P, PACK], F32, name="gain_sb")
         nc.sync.dma_start(out=gain_sb[:], in_=gain.rearrange("(p t) -> p t", t=PACK))
+        gains = keep.tile([P, DATES, PACK], F32, name="gains")
+        nc.scalar.copy(out=gains[:], in_=gain_sb[:].unsqueeze(1).to_broadcast([P, DATES, PACK]))
         nc.sync.dma_start(out=spec_rows[P - N_TILES : P, :], in_=spec.rearrange("(c p) -> c p", p=P))
         tabs = [load_tab(0, shared.tile([P, T], I32, name="tab0", align_bytes=64, offset=0))]
         raws.append(load_w1(1, shared.tile([P, PACK, H], F32, name="w1_raw1", align_bytes=64, offset=3 * STAGE_BYTES)))
 
-        for q in range(4):
-            nc.gpsimd.dma_start(
-                out=w4_plane[32 * q : 32 * q + 4, :].bitcast(I32),
-                in_=w4_scales[0, 4 * q : 4 * q + 4, :].bitcast(I32),
-            )
-
-        gains = keep.tile([P, DATES, PACK], F32, name="gains")
-        nc.scalar.copy(out=gains[:], in_=gain_sb[:].unsqueeze(1).to_broadcast([P, DATES, PACK]))
 
         spec_bank = psum.tile([P, P], F32, name="spec_bank", tag="bank7")
         nc.tensor.transpose(spec_bank[:], spec_rows[:], identity[:])
@@ -149,13 +144,20 @@ def tile_list_shock_factor_vols_kernel(tc, tab_words, tab_scales, offs, w1, gain
         quantize_w1(1)
         w4_codes = shared.tile([P, N], I32, name="w4_codes", align_bytes=64, offset=3 * STAGE_BYTES)
         nc.sync.dma_start(out=w4_codes[:], in_=w4_words[0].rearrange("p c i -> p (c i)").bitcast(I32))
+        w4_plane = shared.tile([P, N], U8, name="w4_plane", align_bytes=64, offset=3 * STAGE_BYTES + 4 * N)
+        nc.vector.memset(w4_plane[:].bitcast(I32), 0)
+        for q in range(4):
+            nc.sync.dma_start(
+                out=w4_plane[32 * q : 32 * q + 4, :].bitcast(I32),
+                in_=w4_scales[0, 4 * q : 4 * q + 4, :].bitcast(I32),
+            )
         for h in range(HALVES):
             gather_words(1, h * COLS, (h + 1) * COLS)
             for b in range(h * PACK, (h + 1) * PACK):
                 first_product(1, b)
         quantize_w1(2)
 
-        squares = [keep.tile([P, DATES, PACK], F32, name=f"squares{b}", align_bytes=64) for b in range(BANKS)]
+        squares = keep.tile([P, BANKS, DATES * PACK], F32, name="squares", align_bytes=64)
         h_grouped = [keep.tile([P, COLS * PACK], BF16, name="h_grouped0", tag="h_grouped", align_bytes=64)]
         h_codes = [keep.tile([P, COLS], U32, name=f"h_codes{h}", align_bytes=64) for h in range(HALVES)]
         h_planes = [keep.tile([P, COLS], U8, name=f"h_plane{h}", align_bytes=64) for h in range(HALVES)]
@@ -164,14 +166,14 @@ def tile_list_shock_factor_vols_kernel(tc, tab_words, tab_scales, offs, w1, gain
             if b % 2 == 0:
                 gather_words(2, b * DATES, (b + 2) * DATES)
             first_product(2, b)
-            nc.scalar.activation(out=squares[b][:], in_=f_banks[b][:].rearrange("p t j -> p j t"), func=ACT.Square)
+            nc.scalar.activation(out=squares[:, b].rearrange("p (j t) -> p j t", t=PACK), in_=f_banks[b][:].rearrange("p t j -> p j t"), func=ACT.Square)
 
-        def weigh(b, engine):
+        def weigh(b, banks, engine):
             h, i = divmod(b, PACK)
             engine.tensor_tensor(
-                out=h_grouped[h][:, i * COLS : (i + 1) * COLS],
-                in0=squares[b][:].rearrange("p j t -> p (j t)"),
-                in1=gains[:].rearrange("p j t -> p (j t)"),
+                out=h_grouped[h][:, i * COLS : (i + banks) * COLS].rearrange("p (b x) -> p b x", b=banks),
+                in0=squares[:, b : b + banks],
+                in1=gains[:].rearrange("p j t -> p (j t)").unsqueeze(1).to_broadcast([P, banks, COLS]),
                 op=ALU.mult,
             )
 
@@ -183,13 +185,13 @@ def tile_list_shock_factor_vols_kernel(tc, tab_words, tab_scales, offs, w1, gain
             )
 
         for b in range(3):
-            weigh(b, nc.vector)
+            weigh(b, 1, nc.vector)
         quantize_h(0, slice(0, 2 * DATES))
-        weigh(3, nc.vector)
+        weigh(3, 1, nc.vector)
         quantize_h(0, slice(2 * DATES, COLS))
         h_grouped.append(keep.tile([P, COLS * PACK], BF16, name="h_grouped1", tag="h_grouped", align_bytes=64))
-        for b in range(PACK, BANKS):
-            weigh(b, nc.gpsimd)
+        for b in range(PACK, BANKS, 2):
+            weigh(b, 2, nc.gpsimd)
 
         for_scalar, for_vector = [], []
 
@@ -234,17 +236,17 @@ def tile_list_shock_factor_vols_kernel(tc, tab_words, tab_scales, offs, w1, gain
         def larger(y, minus_y, size, cols):
             nc.vector.tensor_tensor(out=size[:, :, cols], in0=y[:, :, cols], in1=minus_y[:, :, cols], op=ALU.max)
 
-        def halve(i):
-            y, size = products(for_vector, BANKS // 2, i, whole)
-            half_y = ring.tile([P, COLS], F32, name="half_y")
-            nc.vector.tensor_scalar_mul(out=half_y[:], in0=y[:, 0], scalar1=0.5)
-            return half_y, size[:, 0]
+        half_y = keep.tile([P, 2, COLS], F32, name="half_y")
 
-        def abs_on_gpsimd(half_y, size):
-            positive = keep.tile([P, COLS], F32, name="positive", tag="h_grouped", align_bytes=64)
+        def halve(i, k):
+            y, size = products(for_vector, BANKS // 2, i + k, whole)
+            nc.vector.tensor_scalar_mul(out=half_y[:, k], in0=y[:, 0], scalar1=0.5)
+
+        def abs_on_gpsimd(i):
+            positive = keep.tile([P, 2, COLS], F32, name="positive", tag="h_grouped", align_bytes=64)
             nc.gpsimd.tensor_scalar(out=positive[:], in0=half_y[:], scalar1=LARGEST, scalar2=0.0, op0=ALU.min, op1=ALU.max)
             nc.gpsimd.tensor_scalar(out=positive[:], in0=positive[:], scalar1=2.0, scalar2=0.0, op0=ALU.mult, op1=ALU.add)
-            nc.gpsimd.tensor_tensor(out=size, in0=positive[:], in1=half_y[:], op=ALU.subtract)
+            nc.gpsimd.tensor_tensor(out=vols[:, i : i + 2], in0=positive[:], in1=half_y[:], op=ALU.subtract)
 
         def finish(i, cols, scale=1.0):
             h, c = divmod(i, N_TILES)
@@ -258,33 +260,31 @@ def tile_list_shock_factor_vols_kernel(tc, tab_words, tab_scales, offs, w1, gain
         larger(*made, chunks[0])
         finish(0, whole)
         finish(1, whole)
-        groups = ((1, 2, 0), (0, 2, 1), (1, 0, 1), (1, 2, 0), (1, 1, 1), (1, 2, 0), (0, 2, 0))
-        i = 4
+        slow = N_TILES - 2
         waiting = [2, 3]
-        slow = [[], []]
-        for g, (own, other, third) in enumerate(groups):
-            scalars = range(i, i + own)
-            vectors = range(i + own, i + own + other)
-            gpsimds = range(i + own + other, i + own + other + third)
-            i = i + own + other + third
-            halved = [halve(k) for k in gpsimds]
-            negated = [negate(k, whole) for k in vectors]
-            for k in scalars:
-                abs_on_scalar(k, whole)
-            if g == 1:
+        for i in (4, 7, 12, 15, 18):
+            if i == 7:
+                halve(slow, 0)
+                halve(slow, 1)
+            negated = [negate(i + 1, whole), negate(i + 2, whole)]
+            abs_on_scalar(i, whole)
+            if i == 7:
                 quantize_h(1, whole)
-            for made in halved:
-                abs_on_gpsimd(*made)
-            for k in waiting:
+                abs_on_gpsimd(slow)
+            for k in waiting + [i]:
                 finish(k, whole)
-            for k in scalars:
-                finish(k, whole)
-            for k in slow.pop(0):
-                finish(k, whole, 2.0)
-            slow.append(gpsimds)
-            waiting = list(vectors)
+            waiting = [i + 1, i + 2]
             for made in negated:
                 larger(*made, whole)
+        negated = [negate(21, whole), negate(22, whole)]
+        for k in waiting:
+            finish(k, whole)
+        finish(slow, whole, 2.0)
+        finish(slow + 1, whole, 2.0)
+        for made in negated:
+            larger(*made, whole)
+        waiting = [21, 22]
+        i = 23
         y, size = products(for_vector, BANKS // 2, i, whole)
         minus_y = ring.tile([P, 1, COLS], F32, name="minus_y")
         for cols in chunks:

@@ -30,6 +30,10 @@ FIRST_ROW = P - SCALE_ROWS
 LAST_ROWS = P - 16
 STAGE_BYTES = 4 * T
 LARGEST = 3.4028234663852886e38
+GROUP = 3
+ROOT_OF_SLOW = (19, 22)
+OWN_AFTER = {4: 3, 7: 6, 8: 9, 14: 12, 16: 15, 19: 18, 22: 21}
+HELD = 5
 VECTOR_SHARE = (48, 48, 72)
 
 
@@ -159,14 +163,18 @@ def tile_list_shock_factor_vols_kernel(tc, tab_words, tab_scales, offs, w1, gain
 
         squares = keep.tile([P, BANKS, DATES * PACK], F32, name="squares", align_bytes=64)
         h_grouped = [keep.tile([P, COLS * PACK], BF16, name="h_grouped0", tag="h_grouped", align_bytes=64)]
-        h_codes = [keep.tile([P, COLS], U32, name=f"h_codes{h}", align_bytes=64) for h in range(HALVES)]
+        h_codes = [keep.tile([P, COLS], U32, name="h_codes0", align_bytes=64)]
         h_planes = [keep.tile([P, COLS], U8, name=f"h_plane{h}", align_bytes=64) for h in range(HALVES)]
+
+        def square(b):
+            nc.scalar.activation(out=squares[:, b].rearrange("p (j t) -> p j t", t=PACK), in_=f_banks[b][:].rearrange("p t j -> p j t"), func=ACT.Square)
 
         for b in range(BANKS):
             if b % 2 == 0:
                 gather_words(2, b * DATES, (b + 2) * DATES)
             first_product(2, b)
-            nc.scalar.activation(out=squares[:, b].rearrange("p (j t) -> p j t", t=PACK), in_=f_banks[b][:].rearrange("p t j -> p j t"), func=ACT.Square)
+            if b < BANKS - 1:
+                square(b)
 
         def weigh(b, banks, engine):
             h, i = divmod(b, PACK)
@@ -190,8 +198,7 @@ def tile_list_shock_factor_vols_kernel(tc, tab_words, tab_scales, offs, w1, gain
         weigh(3, 1, nc.vector)
         quantize_h(0, slice(2 * DATES, COLS))
         h_grouped.append(keep.tile([P, COLS * PACK], BF16, name="h_grouped1", tag="h_grouped", align_bytes=64))
-        for b in range(PACK, BANKS, 2):
-            weigh(b, 2, nc.gpsimd)
+        weigh(PACK, 2, nc.gpsimd)
 
         for_scalar, for_vector = [], []
 
@@ -229,18 +236,21 @@ def tile_list_shock_factor_vols_kernel(tc, tab_words, tab_scales, offs, w1, gain
 
         def negate(i, cols):
             y, size = products(for_vector, BANKS // 2, i, cols)
-            minus_y = ring.tile(list(y.shape), F32, name="minus_y")
+            if i == HELD:
+                minus_y = keep.tile(list(y.shape), F32, name="minus_y_held", tag="h_codes1", align_bytes=64)
+            else:
+                minus_y = ring.tile(list(y.shape), F32, name="minus_y")
             nc.vector.tensor_scalar_mul(out=minus_y[:], in0=y, scalar1=-1.0)
             return y, minus_y[:], size
 
         def larger(y, minus_y, size, cols):
-            nc.vector.tensor_tensor(out=size[:, :, cols], in0=y[:, :, cols], in1=minus_y[:, :, cols], op=ALU.max)
+            nc.vector.tensor_tensor(out=size[:, :, cols], in0=minus_y[:, :, cols], in1=y[:, :, cols], op=ALU.max)
 
         half_y = keep.tile([P, 2, COLS], F32, name="half_y")
 
-        def halve(i, k):
-            y, size = products(for_vector, BANKS // 2, i + k, whole)
-            nc.vector.tensor_scalar_mul(out=half_y[:, k], in0=y[:, 0], scalar1=0.5)
+        def halve(i, cols):
+            y, size = products(for_vector, BANKS // 2, i, cols)
+            nc.vector.tensor_scalar_mul(out=half_y[:, :, cols], in0=y, scalar1=0.5)
 
         def abs_on_gpsimd(i):
             positive = keep.tile([P, 2, COLS], F32, name="positive", tag="h_grouped", align_bytes=64)
@@ -253,44 +263,48 @@ def tile_list_shock_factor_vols_kernel(tc, tab_words, tab_scales, offs, w1, gain
             nc.scalar.activation(out=vols[:, i, cols], in_=vols[:, i, cols], func=ACT.Sqrt, bias=spec_sb[:, c : c + 1], scale=scale)
             nc.sync.dma_start(out=out[c * P : (c + 1) * P, h * COLS + cols.start : h * COLS + cols.stop], in_=vols[:, i, cols])
 
-        abs_on_scalar(0, chunks[0])
-        abs_on_scalar(2, chunks[0])
-        made = negate(2, chunks[1])
-        abs_on_scalar(0, chunks[1])
-        larger(*made, chunks[0])
-        finish(0, whole)
-        finish(1, whole)
         slow = N_TILES - 2
-        waiting = [2, 3]
-        for i in (4, 7, 12, 15, 18):
-            if i == 7:
-                halve(slow, 0)
-                halve(slow, 1)
-            negated = [negate(i + 1, whole), negate(i + 2, whole)]
-            abs_on_scalar(i, whole)
-            if i == 7:
+        last = HALVES * N_TILES - 1
+        abs_on_scalar(0, chunks[0])
+        halve(slow, chunks[0])
+        finish(0, chunks[0])
+        finish(1, chunks[0])
+        square(BANKS - 1)
+        weigh(PACK + 2, 2, nc.gpsimd)
+        halve(slow, chunks[1])
+        ahead = (2, negate(2, whole))
+        abs_on_scalar(0, chunks[1])
+        finish(0, chunks[1])
+        finish(1, chunks[1])
+
+        ready = []
+        for i in range(3, last):
+            if i % GROUP == 0 or i in (slow, slow + 1):
+                continue
+            made, ahead = ahead, (i, negate(i, whole))
+            if i == slow - 2:
+                h_codes.append(keep.tile([P, COLS], U32, name="h_codes1", tag="h_codes1", align_bytes=64))
                 quantize_h(1, whole)
                 abs_on_gpsimd(slow)
-            for k in waiting + [i]:
+            own = OWN_AFTER.get(i)
+            if own is not None:
+                abs_on_scalar(own, whole)
+            larger(*made[1], whole)
+            for k in ready:
                 finish(k, whole)
-            waiting = [i + 1, i + 2]
-            for made in negated:
-                larger(*made, whole)
-        negated = [negate(21, whole), negate(22, whole)]
-        for k in waiting:
-            finish(k, whole)
-        finish(slow, whole, 2.0)
-        finish(slow + 1, whole, 2.0)
-        for made in negated:
-            larger(*made, whole)
-        waiting = [21, 22]
-        i = 23
-        y, size = products(for_vector, BANKS // 2, i, whole)
+            ready = [made[0]]
+            if own is not None:
+                finish(own, whole)
+            if i in ROOT_OF_SLOW:
+                finish(slow + ROOT_OF_SLOW.index(i), whole, 2.0)
+        y, size = products(for_vector, BANKS // 2, last, whole)
         minus_y = ring.tile([P, 1, COLS], F32, name="minus_y")
-        for cols in chunks:
-            nc.vector.tensor_scalar_mul(out=minus_y[:, :, cols], in0=y[:, :, cols], scalar1=-1.0)
-        for k in waiting:
+        nc.vector.tensor_scalar_mul(out=minus_y[:, :, chunks[0]], in0=y[:, :, chunks[0]], scalar1=-1.0)
+        larger(*ahead[1], whole)
+        nc.vector.tensor_scalar_mul(out=minus_y[:, :, chunks[1]], in0=y[:, :, chunks[1]], scalar1=-1.0)
+        for k in ready:
             finish(k, whole)
+        finish(ahead[0], whole)
         for cols in chunks:
             larger(y, minus_y[:], size, cols)
-            finish(i, cols)
+            finish(last, cols)

@@ -30,10 +30,10 @@ FIRST_ROW = P - SCALE_ROWS
 LAST_ROWS = P - 16
 STAGE_BYTES = 4 * T
 LARGEST = 3.4028234663852886e38
-GROUP = 3
-ROOT_OF_SLOW = (19, 22)
-OWN_AFTER = {4: 3, 7: 6, 8: 9, 14: 12, 16: 15, 19: 18, 22: 21}
-HELD = 5
+SCALAR_BANKS = (0, 1)
+VECTOR_BANKS = (2, 3, 4, 5, 6, 7)
+SLOW = (10, 11, 22)
+HELD = 6
 VECTOR_SHARE = (48, 48, 72)
 
 
@@ -200,11 +200,7 @@ def tile_list_shock_factor_vols_kernel(tc, tab_words, tab_scales, offs, w1, gain
         h_grouped.append(keep.tile([P, COLS * PACK], BF16, name="h_grouped1", tag="h_grouped", align_bytes=64))
         weigh(PACK, 2, nc.gpsimd)
 
-        for_scalar, for_vector = [], []
-
-        def new_bank(made, first_bank):
-            made.append(psum.tile([P, COLS], F32, name=f"y{first_bank}_{len(made)}", tag=f"bank{first_bank + len(made) % (BANKS // 2)}"))
-            return made[-1]
+        made = {"scalar": 0, "vector": 0}
 
         def second_product(y, i, cols):
             h, c = divmod(i, N_TILES)
@@ -221,90 +217,105 @@ def tile_list_shock_factor_vols_kernel(tc, tab_words, tab_scales, offs, w1, gain
         vols = keep.tile([P, HALVES * N_TILES, COLS], F32, name="vols")
         whole = slice(0, COLS)
         chunks = (slice(0, COLS // 2), slice(COLS // 2, COLS))
+        out_rows = out.rearrange("(c p) j -> p c j", p=P)
 
-        def products(made, first_bank, i, cols):
-            y = new_bank(made, first_bank)
+        def products(reader, banks, i, cols):
+            bank = banks[made[reader] % len(banks)]
+            y = psum.tile([P, COLS], F32, name=f"y_{reader}{made[reader]}", tag=f"bank{bank}")
+            made[reader] = made[reader] + 1
             tiles = COLS // (cols.stop - cols.start)
             view = y[:].rearrange("p (k j) -> p k j", k=tiles)
             for k in range(tiles):
                 second_product(view[:, k], i + k, cols)
             return view, vols[:, i : i + tiles, cols]
 
-        def abs_on_scalar(i, cols):
-            y, size = products(for_scalar, 0, i, cols)
+        def absolute(i, cols=whole):
+            y, size = products("scalar", SCALAR_BANKS, i, cols)
             nc.scalar.activation(out=size, in_=y, func=ACT.Abs)
 
-        def negate(i, cols):
-            y, size = products(for_vector, BANKS // 2, i, cols)
+        negated = {}
+
+        def negate(i, cols=whole):
+            y, size = products("vector", VECTOR_BANKS, i, cols)
             if i == HELD:
                 minus_y = keep.tile(list(y.shape), F32, name="minus_y_held", tag="h_codes1", align_bytes=64)
             else:
                 minus_y = ring.tile(list(y.shape), F32, name="minus_y")
             nc.vector.tensor_scalar_mul(out=minus_y[:], in0=y, scalar1=-1.0)
-            return y, minus_y[:], size
+            negated[i, cols.start] = (y, minus_y[:], size)
 
-        def larger(y, minus_y, size, cols):
-            nc.vector.tensor_tensor(out=size[:, :, cols], in0=minus_y[:, :, cols], in1=y[:, :, cols], op=ALU.max)
+        def larger(i, cols=whole, part=None):
+            y, minus_y, size = negated[i, cols.start]
+            part = part or slice(0, cols.stop - cols.start)
+            nc.vector.tensor_tensor(out=size[:, :, part], in0=minus_y[:, :, part], in1=y[:, :, part], op=ALU.max)
 
-        half_y = keep.tile([P, 2, COLS], F32, name="half_y")
+        half_y = keep.tile([P, len(SLOW), COLS], F32, name="half_y")
 
-        def halve(i, cols):
-            y, size = products(for_vector, BANKS // 2, i, cols)
-            nc.vector.tensor_scalar_mul(out=half_y[:, :, cols], in0=y, scalar1=0.5)
+        def halve(n):
+            y, size = products("vector", VECTOR_BANKS, SLOW[n], whole)
+            nc.vector.tensor_scalar_mul(out=half_y[:, n : n + 1], in0=y, scalar1=0.5)
 
-        def abs_on_gpsimd(i):
-            positive = keep.tile([P, 2, COLS], F32, name="positive", tag="h_grouped", align_bytes=64)
-            nc.gpsimd.tensor_scalar(out=positive[:], in0=half_y[:], scalar1=LARGEST, scalar2=0.0, op0=ALU.min, op1=ALU.max)
+        def abs_on_gpsimd(n, tiles):
+            positive = keep.tile([P, tiles, COLS], F32, name=f"positive{n}", tag="h_grouped", align_bytes=64)
+            halves = half_y[:, n : n + tiles]
+            nc.gpsimd.tensor_scalar(out=positive[:], in0=halves, scalar1=LARGEST, scalar2=0.0, op0=ALU.min, op1=ALU.max)
             nc.gpsimd.tensor_scalar(out=positive[:], in0=positive[:], scalar1=2.0, scalar2=0.0, op0=ALU.mult, op1=ALU.add)
-            nc.gpsimd.tensor_tensor(out=vols[:, i : i + 2], in0=positive[:], in1=half_y[:], op=ALU.subtract)
+            nc.gpsimd.tensor_tensor(out=vols[:, SLOW[n] : SLOW[n] + tiles], in0=positive[:], in1=halves, op=ALU.subtract)
 
-        def finish(i, cols, scale=1.0):
+        def store(i, tiles, cols):
             h, c = divmod(i, N_TILES)
+            dates = slice(h * COLS + cols.start, h * COLS + cols.stop)
+            nc.sync.dma_start(out=out_rows[:, c : c + tiles, dates], in_=vols[:, i : i + tiles, cols])
+
+        def root(i, cols=whole):
+            c = i % N_TILES
+            scale = 2.0 if i in SLOW else 1.0
             nc.scalar.activation(out=vols[:, i, cols], in_=vols[:, i, cols], func=ACT.Sqrt, bias=spec_sb[:, c : c + 1], scale=scale)
-            nc.sync.dma_start(out=out[c * P : (c + 1) * P, h * COLS + cols.start : h * COLS + cols.stop], in_=vols[:, i, cols])
 
-        slow = N_TILES - 2
-        last = HALVES * N_TILES - 1
-        abs_on_scalar(0, chunks[0])
-        halve(slow, chunks[0])
-        finish(0, chunks[0])
-        finish(1, chunks[0])
-        square(BANKS - 1)
-        weigh(PACK + 2, 2, nc.gpsimd)
-        halve(slow, chunks[1])
-        ahead = (2, negate(2, whole))
-        abs_on_scalar(0, chunks[1])
-        finish(0, chunks[1])
-        finish(1, chunks[1])
+        def finish(i):
+            root(i)
+            store(i, 1, whole)
 
-        ready = []
-        for i in range(3, last):
-            if i % GROUP == 0 or i in (slow, slow + 1):
-                continue
-            made, ahead = ahead, (i, negate(i, whole))
-            if i == slow - 2:
-                h_codes.append(keep.tile([P, COLS], U32, name="h_codes1", tag="h_codes1", align_bytes=64))
-                quantize_h(1, whole)
-                abs_on_gpsimd(slow)
-            own = OWN_AFTER.get(i)
-            if own is not None:
-                abs_on_scalar(own, whole)
-            larger(*made[1], whole)
-            for k in ready:
-                finish(k, whole)
-            ready = [made[0]]
-            if own is not None:
-                finish(own, whole)
-            if i in ROOT_OF_SLOW:
-                finish(slow + ROOT_OF_SLOW.index(i), whole, 2.0)
-        y, size = products(for_vector, BANKS // 2, last, whole)
-        minus_y = ring.tile([P, 1, COLS], F32, name="minus_y")
-        nc.vector.tensor_scalar_mul(out=minus_y[:, :, chunks[0]], in0=y[:, :, chunks[0]], scalar1=-1.0)
-        larger(*ahead[1], whole)
-        nc.vector.tensor_scalar_mul(out=minus_y[:, :, chunks[1]], in0=y[:, :, chunks[1]], scalar1=-1.0)
-        for k in ready:
-            finish(k, whole)
-        finish(ahead[0], whole)
-        for cols in chunks:
-            larger(y, minus_y[:], size, cols)
-            finish(last, cols)
+        def finish_first(cols):
+            root(0, cols)
+            root(1, cols)
+            store(0, 2, cols)
+
+        def last_square():
+            square(BANKS - 1)
+            weigh(PACK + 2, 2, nc.gpsimd)
+
+        def second_half():
+            h_codes.append(keep.tile([P, COLS], U32, name="h_codes1", tag="h_codes1", align_bytes=64))
+            quantize_h(1, whole)
+            abs_on_gpsimd(0, 2)
+
+        def last_slow():
+            halve(2)
+            abs_on_gpsimd(2, 1)
+
+        def finish_last():
+            for cols in chunks:
+                root(23, cols)
+                store(23, 1, cols)
+
+        def larger_last():
+            for cols in chunks:
+                larger(23, whole, cols)
+
+        on_vector = [
+            (negate, 2, chunks[0]), (negate, 2, chunks[1]), (larger, 2, chunks[0]), (larger, 2, chunks[1]),
+            (negate, 5), (negate, 6), (larger, 5), (halve, 0), (larger, 6), (halve, 1), (second_half,),
+            (negate, 9), (negate, 12), (larger, 9), (negate, 14), (larger, 12), (negate, 15), (larger, 14), (negate, 17), (larger, 15),
+            (last_slow,), (negate, 18), (larger, 17), (negate, 20), (larger, 18), (negate, 21), (larger, 20), (negate, 23), (larger, 21), (larger_last,),
+        ]
+        on_scalar = [
+            (absolute, 0, chunks[0]), (last_square,), (finish_first, chunks[0]), (absolute, 0, chunks[1]), (absolute, 4), (finish_first, chunks[1]),
+            (finish, 2), (finish, 3), (finish, 4), (finish, 5), (absolute, 7), (finish, 6), (absolute, 8), (finish, 7), (finish, 8),
+            (absolute, 13), (finish, 9), (finish, 13), (finish, 12), (absolute, 16), (finish, 14), (finish, 16), (finish, 15),
+            (finish, 10), (finish, 11), (finish, 17), (absolute, 19), (finish, 18), (finish, 19), (finish, 20), (finish, 22), (finish, 21), (finish_last,),
+        ]
+        for n in range(len(on_scalar)):
+            on_scalar[n][0](*on_scalar[n][1:])
+            if n < len(on_vector):
+                on_vector[n][0](*on_vector[n][1:])

@@ -32,7 +32,7 @@ STAGE_BYTES = 4 * T
 LARGEST = 3.4028234663852886e38
 SCALAR_BANKS = (0, 1)
 VECTOR_BANKS = (2, 3, 4, 5, 6, 7)
-SLOW = (10, 11, 22)
+SLOW = (11, 15, 19)
 HELD = 6
 VECTOR_SHARE = (48, 48, 72)
 
@@ -249,18 +249,17 @@ def tile_list_shock_factor_vols_kernel(tc, tab_words, tab_scales, offs, w1, gain
             part = part or slice(0, cols.stop - cols.start)
             nc.vector.tensor_tensor(out=size[:, :, part], in0=minus_y[:, :, part], in1=y[:, :, part], op=ALU.max)
 
-        half_y = keep.tile([P, len(SLOW), COLS], F32, name="half_y")
+        copied = keep.tile([P, len(SLOW), COLS], F32, name="copied")
 
-        def halve(n):
+        def copy_out(n):
             y, size = products("vector", VECTOR_BANKS, SLOW[n], whole)
-            nc.vector.tensor_scalar_mul(out=half_y[:, n : n + 1], in0=y, scalar1=0.5)
+            nc.vector.tensor_copy(out=copied[:, n : n + 1], in_=y)
 
-        def abs_on_gpsimd(n, tiles):
-            positive = keep.tile([P, tiles, COLS], F32, name=f"positive{n}", tag="h_grouped", align_bytes=64)
-            halves = half_y[:, n : n + tiles]
-            nc.gpsimd.tensor_scalar(out=positive[:], in0=halves, scalar1=LARGEST, scalar2=0.0, op0=ALU.min, op1=ALU.max)
-            nc.gpsimd.tensor_scalar(out=positive[:], in0=positive[:], scalar1=2.0, scalar2=0.0, op0=ALU.mult, op1=ALU.add)
-            nc.gpsimd.tensor_tensor(out=vols[:, SLOW[n] : SLOW[n] + tiles], in0=positive[:], in1=halves, op=ALU.subtract)
+        def abs_on_gpsimd(n):
+            positive = keep.tile([P, 2, COLS], F32, name=f"positive{n}", tag="h_grouped", align_bytes=64)
+            nc.gpsimd.tensor_scalar(out=positive[:, 0], in0=copied[:, n], scalar1=LARGEST, scalar2=0.0, op0=ALU.min, op1=ALU.max)
+            nc.gpsimd.tensor_scalar(out=positive[:, 1], in0=copied[:, n], scalar1=0.0, scalar2=-LARGEST, op0=ALU.min, op1=ALU.max)
+            nc.gpsimd.tensor_tensor(out=vols[:, SLOW[n]], in0=positive[:, 0], in1=positive[:, 1], op=ALU.subtract)
 
         def store(i, tiles, cols):
             h, c = divmod(i, N_TILES)
@@ -269,8 +268,7 @@ def tile_list_shock_factor_vols_kernel(tc, tab_words, tab_scales, offs, w1, gain
 
         def root(i, cols=whole):
             c = i % N_TILES
-            scale = 2.0 if i in SLOW else 1.0
-            nc.scalar.activation(out=vols[:, i, cols], in_=vols[:, i, cols], func=ACT.Sqrt, bias=spec_sb[:, c : c + 1], scale=scale)
+            nc.scalar.activation(out=vols[:, i, cols], in_=vols[:, i, cols], func=ACT.Sqrt, bias=spec_sb[:, c : c + 1])
 
         def finish(i):
             root(i)
@@ -288,11 +286,11 @@ def tile_list_shock_factor_vols_kernel(tc, tab_words, tab_scales, offs, w1, gain
         def second_half():
             h_codes.append(keep.tile([P, COLS], U32, name="h_codes1", tag="h_codes1", align_bytes=64))
             quantize_h(1, whole)
-            abs_on_gpsimd(0, 2)
+            abs_on_gpsimd(0)
 
-        def last_slow():
-            halve(2)
-            abs_on_gpsimd(2, 1)
+        def slow(n):
+            copy_out(n)
+            abs_on_gpsimd(n)
 
         def finish_last():
             for cols in chunks:
@@ -305,15 +303,19 @@ def tile_list_shock_factor_vols_kernel(tc, tab_words, tab_scales, offs, w1, gain
 
         on_vector = [
             (negate, 2, chunks[0]), (negate, 2, chunks[1]), (larger, 2, chunks[0]), (larger, 2, chunks[1]),
-            (negate, 5), (negate, 6), (larger, 5), (halve, 0), (larger, 6), (halve, 1), (second_half,),
-            (negate, 9), (negate, 12), (larger, 9), (negate, 14), (larger, 12), (negate, 15), (larger, 14), (negate, 17), (larger, 15),
-            (last_slow,), (negate, 18), (larger, 17), (negate, 20), (larger, 18), (negate, 21), (larger, 20), (negate, 23), (larger, 21), (larger_last,),
+            (negate, 5), (negate, 6), (larger, 5), (copy_out, 0), (larger, 6), (second_half,),
+            (negate, 9), (negate, 10), (larger, 9), (negate, 13), (larger, 10),
+            (slow, 1), (negate, 14), (larger, 13), (negate, 17), (larger, 14),
+            (slow, 2), (negate, 18), (larger, 17), (negate, 21), (larger, 18),
+            (negate, 22), (larger, 21), (negate, 23), (larger, 22), (larger_last,),
         ]
         on_scalar = [
             (absolute, 0, chunks[0]), (last_square,), (finish_first, chunks[0]), (absolute, 0, chunks[1]), (absolute, 4), (finish_first, chunks[1]),
             (finish, 2), (finish, 3), (finish, 4), (finish, 5), (absolute, 7), (finish, 6), (absolute, 8), (finish, 7), (finish, 8),
-            (absolute, 13), (finish, 9), (finish, 13), (finish, 12), (absolute, 16), (finish, 14), (finish, 16), (finish, 15),
-            (finish, 10), (finish, 11), (finish, 17), (absolute, 19), (finish, 18), (finish, 19), (finish, 20), (finish, 22), (finish, 21), (finish_last,),
+            (finish, 9), (absolute, 12), (finish, 10), (finish, 12), (finish, 11),
+            (finish, 13), (absolute, 16), (finish, 14), (finish, 16), (finish, 15),
+            (finish, 17), (absolute, 20), (finish, 18), (finish, 20), (finish, 21),
+            (finish, 19), (finish, 22), (finish_last,),
         ]
         for n in range(len(on_scalar)):
             on_scalar[n][0](*on_scalar[n][1:])

@@ -34,7 +34,8 @@ SCALAR_BANKS = (0, 1)
 VECTOR_BANKS = (2, 3, 4, 5, 6, 7)
 SLOW = (11, 15, 19)
 HELD = 6
-VECTOR_SHARE = (48, 48, 72)
+W4_COLS = N // 4
+VECTOR_SHARE = (0, 48, 72)
 
 
 def tile_list_shock_factor_vols_kernel(tc, tab_words, tab_scales, offs, w1, gain, w4_words, w4_scales, spec, out):
@@ -45,6 +46,9 @@ def tile_list_shock_factor_vols_kernel(tc, tab_words, tab_scales, offs, w1, gain
         shared = ctx.enter_context(tc.tile_pool(name="shared", bufs=1))
         psum = ctx.enter_context(tc.psum_pool(name="psum", bufs=1))
 
+        w1_rows = w1.rearrange("(a p j) c -> a p j c", p=P, j=PACK)
+        raws = [keep.tile([P, PACK, H], F32, name="w1_raw0")]
+        nc.sync.dma_start(out=raws[0][:, 0:2], in_=w1_rows[0][:, 0:2])
         offsets = keep.tile([P, S // 16], U16, name="offsets")
         nc.sync.dma_start(offsets[:], offs)
 
@@ -68,7 +72,7 @@ def tile_list_shock_factor_vols_kernel(tc, tab_words, tab_scales, offs, w1, gain
         nc.sync.dma_start(out=tab_plane[LAST_ROWS:P, :].bitcast(I32), in_=tab_scales[2].bitcast(I32))
         nc.vector.memset(tab_plane[0:64, :].bitcast(I32), 0)
         nc.vector.memset(tab_plane[64:FIRST_ROW, :].bitcast(I32), 0)
-        v_planes = keep.tile([P, PASSES * S], U8, name="v_planes", align_bytes=64)
+        v_planes = keep.tile([P, 2 * S], U8, name="v_planes", align_bytes=64)
         nc.vector.memset(v_planes[:].bitcast(I32), 0)
 
         def load_tab(a, tab):
@@ -76,11 +80,10 @@ def tile_list_shock_factor_vols_kernel(tc, tab_words, tab_scales, offs, w1, gain
             return tab
 
         def load_w1(a, raw):
-            rows = w1[a * P * PACK : (a + 1) * P * PACK, :]
-            nc.sync.dma_start(out=raw[:], in_=rows.rearrange("(p j) c -> p j c", j=PACK))
+            nc.sync.dma_start(out=raw[:], in_=w1_rows[a])
             return raw
 
-        raws = [load_w1(0, keep.tile([P, PACK, H], F32, name="w1_raw0"))]
+        nc.sync.dma_start(out=raws[0][:, 2:4], in_=w1_rows[0][:, 2:4])
         gain_sb = keep.tile([P, PACK], F32, name="gain_sb")
         nc.sync.dma_start(out=gain_sb[:], in_=gain.rearrange("(p t) -> p t", t=PACK))
         gains = keep.tile([P, DATES, PACK], F32, name="gains")
@@ -98,18 +101,11 @@ def tile_list_shock_factor_vols_kernel(tc, tab_words, tab_scales, offs, w1, gain
         picked = keep.tile([P, S], U8, name="picked", align_bytes=64)
         nc.vector.tensor_copy(out=picked[:], in_=tab_plane[:].indirect(offsets[:]))
 
-        def move_planes(first_row, passes, first_pass):
-            for q in range(4):
-                row = first_row + 4 * passes * q
-                nc.sync.dma_start(
-                    out=v_planes[32 * q : 32 * q + 4, first_pass * S : (first_pass + passes) * S].bitcast(I32),
-                    in_=picked[row : row + 4 * passes, :].bitcast(I32),
-                )
-
-        move_planes(FIRST_ROW, 2, 0)
+        for q in (0, 2, 1, 3):
+            row = FIRST_ROW + 8 * q
+            nc.sync.dma_start(out=v_planes[32 * q : 32 * q + 4, :].bitcast(I32), in_=picked[row : row + 8, :].bitcast(I32))
         tabs.append(load_tab(1, shared.tile([P, T], I32, name="tab1", align_bytes=64, offset=STAGE_BYTES)))
         raws.append(load_w1(2, shared.tile([P, PACK, H], F32, name="w1_raw2", align_bytes=64, offset=2 * STAGE_BYTES)))
-        move_planes(LAST_ROWS, 1, 2)
 
         grouped = [keep.tile([P, H * PACK], BF16, name=f"w1_grouped{a}", align_bytes=64) for a in range(PASSES)]
         w1_codes = [keep.tile([P, H], U32, name=f"w1_codes{a}", align_bytes=64) for a in range(PASSES)]
@@ -125,7 +121,8 @@ def tile_list_shock_factor_vols_kernel(tc, tab_words, tab_scales, offs, w1, gain
             src = raws[a][:].rearrange("p j (m t) -> p m j t", t=PACK)
             cut = VECTOR_SHARE[a]
             nc.scalar.copy(out=dst[:, cut:P], in_=src[:, cut:P])
-            nc.vector.tensor_copy(out=dst[:, 0:cut], in_=src[:, 0:cut])
+            if cut:
+                nc.vector.tensor_copy(out=dst[:, 0:cut], in_=src[:, 0:cut])
             nc.vector.quantize_mx(out=w1_codes[a][:].bitcast(E4M3), scales=w1_planes[a][:], in_=grouped[a][:])
 
         def first_product(a, b):
@@ -135,30 +132,31 @@ def tile_list_shock_factor_vols_kernel(tc, tab_words, tab_scales, offs, w1, gain
                     lhsT=w1_codes[a][:, t * P : (t + 1) * P].bitcast(E4M3),
                     lhsT_scale=w1_planes[a][:, t * P : (t + 1) * P],
                     rhs=v_codes[a][:, b * DATES : (b + 1) * DATES].bitcast(E5M2),
-                    rhs_scale=v_planes[:, a * S + b * DATES : a * S + (b + 1) * DATES],
+                    rhs_scale=v_planes[:, a % 2 * S + b * DATES : a % 2 * S + (b + 1) * DATES],
                     start=(a == 0 and t == 0),
                     stop=(a == PASSES - 1 and t == PACK - 1),
                 )
 
-        gather_words(0, 0, S)
-        tabs.append(load_tab(2, shared.tile([P, T], I32, name="tab2", align_bytes=64, offset=0)))
+        gather_words(0, 0, COLS)
         quantize_w1(0)
+        gather_words(0, COLS, S)
+        tabs.append(load_tab(2, shared.tile([P, T], I32, name="tab2", align_bytes=64, offset=0)))
         for b in range(BANKS):
             first_product(0, b)
+        for r in range(4):
+            nc.sync.dma_start(out=v_planes[r:P:32, 0:S].bitcast(I32), in_=picked[LAST_ROWS + r : P : 4, :].bitcast(I32))
         quantize_w1(1)
-        w4_codes = shared.tile([P, N], I32, name="w4_codes", align_bytes=64, offset=3 * STAGE_BYTES)
-        nc.sync.dma_start(out=w4_codes[:], in_=w4_words[0].rearrange("p c i -> p (c i)").bitcast(I32))
-        w4_plane = shared.tile([P, N], U8, name="w4_plane", align_bytes=64, offset=3 * STAGE_BYTES + 4 * N)
-        nc.vector.memset(w4_plane[:].bitcast(I32), 0)
-        for q in range(4):
-            nc.sync.dma_start(
-                out=w4_plane[32 * q : 32 * q + 4, :].bitcast(I32),
-                in_=w4_scales[0, 4 * q : 4 * q + 4, :].bitcast(I32),
-            )
         for h in range(HALVES):
             gather_words(1, h * COLS, (h + 1) * COLS)
             for b in range(h * PACK, (h + 1) * PACK):
                 first_product(1, b)
+        w4_codes = shared.tile([P, N], I32, name="w4_codes", align_bytes=64, offset=STAGE_BYTES)
+        nc.sync.dma_start(out=w4_codes[:], in_=w4_words[0].rearrange("p c i -> p (c i)").bitcast(I32))
+        w4_plane = shared.tile([P, W4_COLS], U8, name="w4_plane", align_bytes=64, offset=3 * STAGE_BYTES)
+        nc.vector.memset(w4_plane[:].bitcast(I32), 0)
+        for q in range(4):
+            rows = w4_scales[0, 4 * q : 4 * q + 4, :].rearrange("r (g c) -> g r c", g=4)
+            nc.sync.dma_start(out=w4_plane[32 * q : 32 * q + 16, :].bitcast(I32), in_=rows.bitcast(I32))
         quantize_w1(2)
 
         squares = keep.tile([P, BANKS, DATES * PACK], F32, name="squares", align_bytes=64)
@@ -207,7 +205,7 @@ def tile_list_shock_factor_vols_kernel(tc, tab_words, tab_scales, offs, w1, gain
             nc.tensor.matmul_mx(
                 out=y,
                 lhsT=w4_codes[:, c * P : (c + 1) * P].bitcast(E4M3),
-                lhsT_scale=w4_plane[:, c * P : (c + 1) * P],
+                lhsT_scale=w4_plane[4 * (c // 3) : P, c % 3 * P : (c % 3 + 1) * P],
                 rhs=h_codes[h][:, cols].bitcast(E4M3),
                 rhs_scale=h_planes[h][:, cols],
                 start=True,

from contextlib import ExitStack

import concourse.mybir as mybir
from concourse.masks import make_identity

K, T, S, H, N = 1536, 2048, 1024, 512, 1536
FLOPS = 2 * K * H * S + 2 * H * N * S

F32 = mybir.dt.float32
BF16 = mybir.dt.bfloat16
I32 = mybir.dt.int32
U32 = mybir.dt.uint32
U16 = mybir.dt.uint16
U8 = mybir.dt.uint8
E4M3 = mybir.dt.float8_e4m3fn_x4
E5M2 = mybir.dt.float8_e5m2_x4
ACT = mybir.ActivationFunctionType
ALU = mybir.AluOpType

P = 128
PACK = 4
PASSES = K // (P * PACK)
BANKS = 8
DATES = S // BANKS
COLS = 512
HALVES = S // COLS
N_TILES = N // P
SCALE_ROWS = 16 * PASSES
FIRST_ROW = P - SCALE_ROWS
LAST_ROWS = P - 16
STAGE_BYTES = 4 * T
LARGEST = 3.4028234663852886e38
SCALAR_BANKS = (0, 1)
VECTOR_BANKS = (2, 3, 4, 5, 6, 7)
SLOW = (11, 15, 19)
HELD = 6
W4_COLS = N // 4
VECTOR_SHARE = (0, 48, 72)


def tile_list_shock_factor_vols_kernel(tc, tab_words, tab_scales, offs, w1, gain, w4_words, w4_scales, spec, out):
    nc = tc.nc
    with ExitStack() as ctx:
        keep = ctx.enter_context(tc.tile_pool(name="keep", bufs=1))
        ring = ctx.enter_context(tc.tile_pool(name="ring", bufs=6))
        shared = ctx.enter_context(tc.tile_pool(name="shared", bufs=1))
        psum = ctx.enter_context(tc.psum_pool(name="psum", bufs=1))

        w1_rows = w1.rearrange("(a p j) c -> a p j c", p=P, j=PACK)
        raws = [keep.tile([P, PACK, H], F32, name="w1_raw0")]
        nc.sync.dma_start(out=raws[0][:, 0:2], in_=w1_rows[0][:, 0:2])
        offsets = keep.tile([P, S // 16], U16, name="offsets")
        nc.sync.dma_start(offsets[:], offs)

        warm = keep.tile([P, 1], F32, name="warm")
        nc.gpsimd.memset(warm[:], 1.0)
        warm_out = keep.tile([P, 1], F32, name="warm_out")
        nc.scalar.activation(out=warm_out[:], in_=warm[:], func=ACT.Sqrt)


        spec_rows = keep.tile([P, P], F32, name="spec_rows")
        nc.gpsimd.memset(spec_rows[0:96, :], 0.0)
        nc.gpsimd.memset(spec_rows[96 : P - N_TILES, :], 0.0)
        identity = keep.tile([P, P], F32, name="identity")
        make_identity(nc, identity[:])

        tab_plane = shared.tile([P, T], U8, name="tab_plane", align_bytes=64, offset=2 * STAGE_BYTES - T // 2)
        nc.sync.dma_start(
            out=tab_plane[FIRST_ROW:LAST_ROWS, :].bitcast(I32),
            in_=tab_scales[0:2].rearrange("a q t -> q a t").bitcast(I32),
        )
        nc.sync.dma_start(out=tab_plane[LAST_ROWS:P, :].bitcast(I32), in_=tab_scales[2].bitcast(I32))
        nc.vector.memset(tab_plane[0:64, :].bitcast(I32), 0)
        nc.vector.memset(tab_plane[64:FIRST_ROW, :].bitcast(I32), 0)
        v_planes = keep.tile([P, 2 * S], U8, name="v_planes", align_bytes=64)
        nc.vector.memset(v_planes[:].bitcast(I32), 0)

        def load_tab(a, tab):
            nc.sync.dma_start(out=tab[:], in_=tab_words[a].rearrange("p t i -> p (t i)").bitcast(I32))
            return tab

        def load_w1(a, raw):
            nc.sync.dma_start(out=raw[:], in_=w1_rows[a])
            return raw

        nc.sync.dma_start(out=raws[0][:, 2:4], in_=w1_rows[0][:, 2:4])
        gain_sb = keep.tile([P, PACK], F32, name="gain_sb")
        nc.sync.dma_start(out=gain_sb[:], in_=gain.rearrange("(p t) -> p t", t=PACK))
        gains = keep.tile([P, DATES, PACK], F32, name="gains")
        nc.scalar.copy(out=gains[:], in_=gain_sb[:].unsqueeze(1).to_broadcast([P, DATES, PACK]))
        nc.sync.dma_start(out=spec_rows[P - N_TILES : P, :], in_=spec.rearrange("(c p) -> c p", p=P))
        tabs = [load_tab(0, shared.tile([P, T], I32, name="tab0", align_bytes=64, offset=0))]
        raws.append(load_w1(1, shared.tile([P, PACK, H], F32, name="w1_raw1", align_bytes=64, offset=3 * STAGE_BYTES)))


        spec_bank = psum.tile([P, P], F32, name="spec_bank", tag="bank7")
        nc.tensor.transpose(spec_bank[:], spec_rows[:], identity[:])
        spec_sb = keep.tile([P, N_TILES], F32, name="spec_sb")
        nc.scalar.copy(out=spec_sb[:], in_=spec_bank[:, P - N_TILES : P])

        picked = keep.tile([P, S], U8, name="picked", align_bytes=64)
        nc.vector.tensor_copy(out=picked[:], in_=tab_plane[:].indirect(offsets[:]))

        for q in (0, 2, 1, 3):
            row = FIRST_ROW + 8 * q
            nc.sync.dma_start(out=v_planes[32 * q : 32 * q + 4, :].bitcast(I32), in_=picked[row : row + 8, :].bitcast(I32))
        tabs.append(load_tab(1, shared.tile([P, T], I32, name="tab1", align_bytes=64, offset=STAGE_BYTES)))
        raws.append(load_w1(2, shared.tile([P, PACK, H], F32, name="w1_raw2", align_bytes=64, offset=2 * STAGE_BYTES)))

        grouped = [keep.tile([P, H * PACK], BF16, name=f"w1_grouped{a}", align_bytes=64) for a in range(PASSES)]
        w1_codes = [keep.tile([P, H], U32, name=f"w1_codes{a}", align_bytes=64) for a in range(PASSES)]
        w1_planes = [keep.tile([P, H], U8, name=f"w1_plane{a}", align_bytes=64) for a in range(PASSES)]
        v_codes = [keep.tile([P, S], U32, name=f"v_codes{a}", align_bytes=64) for a in range(PASSES)]
        f_banks = [psum.tile([P, PACK, DATES], F32, name=f"f{b}", tag=f"bank{b}") for b in range(BANKS)]

        def gather_words(a, j0, j1):
            nc.vector.tensor_copy(out=v_codes[a][:, j0:j1], in_=tabs[a][:].bitcast(U32).indirect(offsets[:, j0 // 16 : j1 // 16]))

        def quantize_w1(a):
            dst = grouped[a][:].rearrange("p (t m j) -> p m j t", t=PACK, j=PACK)
            src = raws[a][:].rearrange("p j (m t) -> p m j t", t=PACK)
            cut = VECTOR_SHARE[a]
            nc.scalar.copy(out=dst[:, cut:P], in_=src[:, cut:P])
            if cut:
                nc.vector.tensor_copy(out=dst[:, 0:cut], in_=src[:, 0:cut])
            nc.vector.quantize_mx(out=w1_codes[a][:].bitcast(E4M3), scales=w1_planes[a][:], in_=grouped[a][:])

        def first_product(a, b):
            for t in range(PACK):
                nc.tensor.matmul_mx(
                    out=f_banks[b][:, t, :],
                    lhsT=w1_codes[a][:, t * P : (t + 1) * P].bitcast(E4M3),
                    lhsT_scale=w1_planes[a][:, t * P : (t + 1) * P],
                    rhs=v_codes[a][:, b * DATES : (b + 1) * DATES].bitcast(E5M2),
                    rhs_scale=v_planes[:, a % 2 * S + b * DATES : a % 2 * S + (b + 1) * DATES],
                    start=(a == 0 and t == 0),
                    stop=(a == PASSES - 1 and t == PACK - 1),
                )

        gather_words(0, 0, COLS)
        quantize_w1(0)
        gather_words(0, COLS, S)
        tabs.append(load_tab(2, shared.tile([P, T], I32, name="tab2", align_bytes=64, offset=0)))
        for b in range(BANKS):
            first_product(0, b)
        for r in range(4):
            nc.sync.dma_start(out=v_planes[r:P:32, 0:S].bitcast(I32), in_=picked[LAST_ROWS + r : P : 4, :].bitcast(I32))
        quantize_w1(1)
        for h in range(HALVES):
            gather_words(1, h * COLS, (h + 1) * COLS)
            for b in range(h * PACK, (h + 1) * PACK):
                first_product(1, b)
        w4_codes = shared.tile([P, N], I32, name="w4_codes", align_bytes=64, offset=STAGE_BYTES)
        nc.sync.dma_start(out=w4_codes[:], in_=w4_words[0].rearrange("p c i -> p (c i)").bitcast(I32))
        w4_plane = shared.tile([P, W4_COLS], U8, name="w4_plane", align_bytes=64, offset=3 * STAGE_BYTES)
        nc.vector.memset(w4_plane[:].bitcast(I32), 0)
        for q in range(4):
            rows = w4_scales[0, 4 * q : 4 * q + 4, :].rearrange("r (g c) -> g r c", g=4)
            nc.sync.dma_start(out=w4_plane[32 * q : 32 * q + 16, :].bitcast(I32), in_=rows.bitcast(I32))
        quantize_w1(2)

        squares = keep.tile([P, BANKS, DATES * PACK], F32, name="squares", align_bytes=64)
        h_grouped = [keep.tile([P, COLS * PACK], BF16, name="h_grouped0", tag="h_grouped", align_bytes=64)]
        h_codes = [keep.tile([P, COLS], U32, name="h_codes0", align_bytes=64)]
        h_planes = [keep.tile([P, COLS], U8, name=f"h_plane{h}", align_bytes=64) for h in range(HALVES)]

        def square(b):
            nc.scalar.activation(out=squares[:, b].rearrange("p (j t) -> p j t", t=PACK), in_=f_banks[b][:].rearrange("p t j -> p j t"), func=ACT.Square)

        for b in range(BANKS):
            if b % 2 == 0:
                gather_words(2, b * DATES, (b + 2) * DATES)
            first_product(2, b)
            if b < BANKS - 1:
                square(b)

        def weigh(b, banks, engine):
            h, i = divmod(b, PACK)
            engine.tensor_tensor(
                out=h_grouped[h][:, i * COLS : (i + banks) * COLS].rearrange("p (b x) -> p b x", b=banks),
                in0=squares[:, b : b + banks],
                in1=gains[:].rearrange("p j t -> p (j t)").unsqueeze(1).to_broadcast([P, banks, COLS]),
                op=ALU.mult,
            )

        def quantize_h(h, cols):
            nc.vector.quantize_mx(
                out=h_codes[h][:, cols].bitcast(E4M3),
                scales=h_planes[h][:, cols],
                in_=h_grouped[h][:, cols.start * PACK : cols.stop * PACK],
            )

        for b in range(3):
            weigh(b, 1, nc.vector)
        quantize_h(0, slice(0, 2 * DATES))
        weigh(3, 1, nc.vector)
        quantize_h(0, slice(2 * DATES, COLS))
        h_grouped.append(keep.tile([P, COLS * PACK], BF16, name="h_grouped1", tag="h_grouped", align_bytes=64))
        weigh(PACK, 2, nc.gpsimd)

        made = {"scalar": 0, "vector": 0}

        def second_product(y, i, cols):
            h, c = divmod(i, N_TILES)
            nc.tensor.matmul_mx(
                out=y,
                lhsT=w4_codes[:, c * P : (c + 1) * P].bitcast(E4M3),
                lhsT_scale=w4_plane[4 * (c // 3) : P, c % 3 * P : (c % 3 + 1) * P],
                rhs=h_codes[h][:, cols].bitcast(E4M3),
                rhs_scale=h_planes[h][:, cols],
                start=True,
                stop=True,
            )

        vols = keep.tile([P, HALVES * N_TILES, COLS], F32, name="vols")
        whole = slice(0, COLS)
        chunks = (slice(0, COLS // 2), slice(COLS // 2, COLS))
        out_rows = out.rearrange("(c p) j -> p c j", p=P)

        def products(reader, banks, i, cols):
            bank = banks[made[reader] % len(banks)]
            y = psum.tile([P, COLS], F32, name=f"y_{reader}{made[reader]}", tag=f"bank{bank}")
            made[reader] = made[reader] + 1
            tiles = COLS // (cols.stop - cols.start)
            view = y[:].rearrange("p (k j) -> p k j", k=tiles)
            for k in range(tiles):
                second_product(view[:, k], i + k, cols)
            return view, vols[:, i : i + tiles, cols]

        def absolute(i, cols=whole):
            y, size = products("scalar", SCALAR_BANKS, i, cols)
            nc.scalar.activation(out=size, in_=y, func=ACT.Abs)

        negated = {}

        def negate(i, cols=whole):
            y, size = products("vector", VECTOR_BANKS, i, cols)
            if i == HELD:
                minus_y = keep.tile(list(y.shape), F32, name="minus_y_held", tag="h_codes1", align_bytes=64)
            else:
                minus_y = ring.tile(list(y.shape), F32, name="minus_y")
            nc.vector.tensor_scalar_mul(out=minus_y[:], in0=y, scalar1=-1.0)
            negated[i, cols.start] = (y, minus_y[:], size)

        def larger(i, cols=whole, part=None):
            y, minus_y, size = negated[i, cols.start]
            part = part or slice(0, cols.stop - cols.start)
            nc.vector.tensor_tensor(out=size[:, :, part], in0=minus_y[:, :, part], in1=y[:, :, part], op=ALU.max)

        copied = keep.tile([P, len(SLOW), COLS], F32, name="copied")

        def copy_out(n):
            y, size = products("vector", VECTOR_BANKS, SLOW[n], whole)
            nc.vector.tensor_copy(out=copied[:, n : n + 1], in_=y)

        def abs_on_gpsimd(n):
            positive = keep.tile([P, 2, COLS], F32, name=f"positive{n}", tag="h_grouped", align_bytes=64)
            nc.gpsimd.tensor_scalar(out=positive[:, 0], in0=copied[:, n], scalar1=LARGEST, scalar2=0.0, op0=ALU.min, op1=ALU.max)
            nc.gpsimd.tensor_scalar(out=positive[:, 1], in0=copied[:, n], scalar1=0.0, scalar2=-LARGEST, op0=ALU.min, op1=ALU.max)
            nc.gpsimd.tensor_tensor(out=vols[:, SLOW[n]], in0=positive[:, 0], in1=positive[:, 1], op=ALU.subtract)

        def store(i, tiles, cols):
            h, c = divmod(i, N_TILES)
            dates = slice(h * COLS + cols.start, h * COLS + cols.stop)
            nc.sync.dma_start(out=out_rows[:, c : c + tiles, dates], in_=vols[:, i : i + tiles, cols])

        def root(i, cols=whole):
            c = i % N_TILES
            nc.scalar.activation(out=vols[:, i, cols], in_=vols[:, i, cols], func=ACT.Sqrt, bias=spec_sb[:, c : c + 1])

        def finish(i):
            root(i)
            store(i, 1, whole)

        def finish_first(cols):
            root(0, cols)
            root(1, cols)
            store(0, 2, cols)

        def last_square():
            square(BANKS - 1)
            weigh(PACK + 2, 2, nc.gpsimd)

        def second_half():
            h_codes.append(keep.tile([P, COLS], U32, name="h_codes1", tag="h_codes1", align_bytes=64))
            quantize_h(1, whole)
            abs_on_gpsimd(0)

        def slow(n):
            copy_out(n)
            abs_on_gpsimd(n)

        def finish_last():
            for cols in chunks:
                root(23, cols)
                store(23, 1, cols)

        def larger_last():
            for cols in chunks:
                larger(23, whole, cols)

        on_vector = [
            (negate, 2, chunks[0]), (negate, 2, chunks[1]), (larger, 2, chunks[0]), (larger, 2, chunks[1]),
            (negate, 5), (negate, 6), (larger, 5), (copy_out, 0), (larger, 6), (second_half,),
            (negate, 9), (negate, 10), (larger, 9), (negate, 13), (larger, 10),
            (slow, 1), (negate, 14), (larger, 13), (negate, 17), (larger, 14),
            (slow, 2), (negate, 18), (larger, 17), (negate, 21), (larger, 18),
            (negate, 22), (larger, 21), (negate, 23), (larger, 22), (larger_last,),
        ]
        on_scalar = [
            (absolute, 0, chunks[0]), (last_square,), (finish_first, chunks[0]), (absolute, 0, chunks[1]), (absolute, 4), (finish_first, chunks[1]),
            (finish, 2), (finish, 3), (finish, 4), (finish, 5), (absolute, 7), (finish, 6), (absolute, 8), (finish, 7), (finish, 8),
            (finish, 9), (absolute, 12), (finish, 10), (finish, 12), (finish, 11),
            (finish, 13), (absolute, 16), (finish, 14), (finish, 16), (finish, 15),
            (finish, 17), (absolute, 20), (finish, 18), (finish, 20), (finish, 21),
            (finish, 19), (finish, 22), (finish_last,),
        ]
        for n in range(len(on_scalar)):
            on_scalar[n][0](*on_scalar[n][1:])
            if n < len(on_vector):
                on_vector[n][0](*on_vector[n][1:])
